import numpy as np
import ml_dtypes


def mxq(x, axis, fmt="e4m3"):
    dtype, down = {"e4m3": (ml_dtypes.float8_e4m3fn, 7), "e5m2": (ml_dtypes.float8_e5m2, 14)}[fmt]
    v = np.moveaxis(np.asarray(x, np.float32).astype(ml_dtypes.bfloat16).astype(np.float64), axis, -1)
    blocks = v.reshape(v.shape[:-1] + (-1, 32))
    amax = np.abs(blocks).max(-1, keepdims=True)
    byte = np.maximum(np.where(amax > 0, np.frexp(amax)[1] - 1 + 127, 0) - down, 1)
    scale = np.exp2(byte - 127.0)
    codes = (blocks / scale).astype(np.float32).astype(dtype).astype(np.float64)
    return np.moveaxis((codes * scale).reshape(v.shape), -1, axis)


WIDE = False


def mx_kscale(k):
    if not WIDE:
        return np.ones(k)
    levels = np.array([10, -10, 5, -5, 0])
    if k % 512:
        return np.exp2(np.random.permutation(np.resize(levels, k // 32))).repeat(32)
    a = np.empty((k // 512, 16))
    for p in range(k // 512):
        a[p, :8] = np.random.permutation(np.resize(levels, 8))
        for g in range(8):
            far = levels[np.abs(levels - a[p, g]) >= 10]
            a[p, g + 8] = far[np.random.randint(len(far))]
    return np.exp2(a.ravel()).repeat(32)


def f64(x):
    return np.asarray(x).astype(np.float64)


def striped(idx):
    return np.tile(idx.reshape(-1, 16).T, (8, 1)).astype(np.uint16)


def unstriped(offs):
    return offs[:16].T.reshape(-1).astype(np.int64)


def pack_weight(w):
    k, n = w.shape
    w = f64(np.asarray(w, np.float32).astype(ml_dtypes.bfloat16)).reshape(k // 32, 32, n)
    amax = np.abs(w).max(1)
    byte = np.clip(np.where(amax > 0, np.frexp(amax)[1] - 1 + 127 - 7, 1), 1, 254)
    scaled = (w * np.exp2(127.0 - byte)[:, None, :]).reshape(k, n).astype(np.float32)
    words = np.ascontiguousarray(scaled.reshape(k // 512, 128, 4, n).transpose(0, 1, 3, 2)).astype(ml_dtypes.float8_e4m3fn).view(np.uint8)
    return words, np.ascontiguousarray(byte.astype(np.uint8).reshape(k // 512, 16, n))


def unpack_weight(words, scales):
    g, p, n, _ = words.shape
    vals = np.ascontiguousarray(words).view(ml_dtypes.float8_e4m3fn).astype(np.float64) * np.repeat(np.exp2(scales.astype(np.float64) - 127.0), 8, axis=1)[..., None]
    return vals.transpose(0, 1, 3, 2).reshape(g * 512, n)


def gelu(v):
    return 0.5 * v * (1.0 + np.tanh(np.sqrt(2.0 / np.pi) * (v + 0.044715 * v**3)))


K, T, S, V, H, N = 512, 4096, 1024, 512, 512, 128


def setup_inputs():
    n = np.random.standard_normal
    s = mx_kscale(K)[:, None]
    u = mx_kscale(H)
    packed_xT = pack_weight(n((K, T)) * s)
    packed_w2 = pack_weight(n((H, N)) / np.sqrt(2 * H) / u[:, None])
    packed_w3 = pack_weight(n((H, N)) / np.sqrt(2 * H) / u[:, None])
    return {
        "x_words": packed_xT[0],
        "x_scales": packed_xT[1],
        "w1": (n((K, H)) / np.sqrt(K) / s * u).astype(np.float32),
        "w2_words": packed_w2[0],
        "w2_scales": packed_w2[1],
        "w3_words": packed_w3[0],
        "w3_scales": packed_w3[1],
        "offs": striped(np.random.permutation(T)[:S]),
    }


def reference(x_words, x_scales, w1, w2_words, w2_scales, w3_words, w3_scales, offs):
    xq = unpack_weight(x_words, x_scales)[:, unstriped(offs)]
    h = gelu(mxq(f64(w1), 0, "e4m3").T @ xq)
    low = 0.5 * (h[:, :V] + h[:, V:2 * V])
    high = 0.5 * (h[:, :V] - h[:, V:2 * V])
    return unpack_weight(w2_words, w2_scales).T @ mxq(low, 0, "e4m3") + unpack_weight(w3_words, w3_scales).T @ mxq(high, 0, "e4m3")

@@ -1,0 +1,167 @@
+from contextlib import ExitStack
+
+import concourse.mybir as mybir
+
+K, T, S, V, H, N = 512, 4096, 1024, 512, 512, 128
+FLOPS = 2 * K * H * S + 2 * 2 * H * N * V
+
+F32 = mybir.dt.float32
+BF16 = mybir.dt.bfloat16
+I32 = mybir.dt.int32
+U32 = mybir.dt.uint32
+U16 = mybir.dt.uint16
+U8 = mybir.dt.uint8
+FP8X4 = mybir.dt.float8_e4m3fn_x4
+ACT = mybir.ActivationFunctionType
+ALU = mybir.AluOpType
+
+P = 128
+PACK = 4
+CHUNK = 128
+HALF = P // 2
+VECTOR_SHARE = 44
+FIRST_WORDS = 1024
+
+
+def load_scale_rows(queue, plane, rows):
+    for r in range(4):
+        queue.dma_start(out=plane[r:P:32, :].bitcast(I32), in_=rows[r:16:4, :].bitcast(I32))
+
+
+def words_of(packed):
+    return packed[0].rearrange("p n t -> p (n t)").bitcast(I32)
+
+
+def tile_picked_haar_gelu_p_kernel(
+    tc, x_words, x_scales, w1, w2_words, w2_scales, w3_words, w3_scales, offs, out
+):
+    nc = tc.nc
+    chunks = V // CHUNK
+    with ExitStack() as ctx:
+        keep = ctx.enter_context(tc.tile_pool(name="keep", bufs=1))
+        stage = ctx.enter_context(tc.tile_pool(name="stage", bufs=2))
+        hidden_psum = ctx.enter_context(tc.psum_pool(name="hidden_psum", bufs=6))
+        out_psum = ctx.enter_context(tc.psum_pool(name="out_psum", bufs=2))
+
+        offsets = keep.tile([P, S // 16], U16, name="offsets")
+        nc.sync.dma_start(offsets[:], offs)
+
+        table_scales = keep.tile([P, T], U8, name="table_scales", align_bytes=64)
+        nc.vector.memset(table_scales[:].bitcast(I32), 0)
+        table_words = keep.tile([P, T], I32, name="table_words", align_bytes=64)
+        nc.sync.dma_start(out=table_words[:, :FIRST_WORDS], in_=words_of(x_words)[:, :FIRST_WORDS])
+        load_scale_rows(nc.sync, table_scales, x_scales[0])
+        nc.sync.dma_start(out=table_words[:, FIRST_WORDS:], in_=words_of(x_words)[:, FIRST_WORDS:])
+
+        w1_rows = w1.rearrange("(p j) c -> p j c", j=PACK)
+        w1_raw = []
+        for half in range(2):
+            raw = stage.tile([P, PACK, H // 2], F32, name=f"w1_raw{half}", tag="staged", align_bytes=64)
+            nc.sync.dma_start(out=raw[:], in_=w1_rows[:, :, half * (H // 2) : (half + 1) * (H // 2)])
+            w1_raw.append(raw)
+
+        band_w_scales = keep.tile([P, 2 * N], U8, name="band_w_scales", align_bytes=64)
+        nc.vector.memset(band_w_scales[:].bitcast(I32), 0)
+        load_scale_rows(nc.sync, band_w_scales[:, 0:N], w2_scales[0])
+        load_scale_rows(nc.sync, band_w_scales[:, N : 2 * N], w3_scales[0])
+
+        picked_scales = keep.tile([P, S], U8, name="picked_scales", align_bytes=64)
+        nc.vector.tensor_copy(picked_scales[:], table_scales[:].indirect(offsets[:]))
+        picked_words = []
+        for d in range(2):
+            picked = keep.tile([P, V], U32, name=f"picked_words{d}", align_bytes=64)
+            piece = offsets[:, d * (V // 16) : (d + 1) * (V // 16)]
+            nc.vector.tensor_copy(picked[:], table_words[:].bitcast(U32).indirect(piece))
+            picked_words.append(picked)
+
+        w1_grouped = [keep.tile([P, PACK, HALF, PACK], BF16, name=f"w1_grouped{half}", align_bytes=64) for half in range(2)]
+
+        def deal(copy, half, m0, m1):
+            src = w1_raw[half][:].rearrange("p j (m t) -> p m t j", t=PACK)[:, m0:m1]
+            dst = w1_grouped[half][:].rearrange("p t m j -> p m t j")[:, m0:m1]
+            copy(dst, src)
+
+        deal(nc.scalar.copy, 0, 0, HALF)
+        deal(nc.vector.tensor_copy, 1, 0, VECTOR_SHARE)
+        deal(nc.scalar.copy, 1, VECTOR_SHARE, HALF)
+
+        w1_codes = keep.tile([P, PACK, P], U32, name="w1_codes", align_bytes=64)
+        w1_scales = keep.tile([P, PACK, P], U8, name="w1_scales", align_bytes=64)
+        for half in range(2):
+            m = slice(half * HALF, (half + 1) * HALF)
+            for t in range(PACK):
+                nc.vector.quantize_mx(
+                    out=w1_codes[:, t, m].bitcast(FP8X4),
+                    scales=w1_scales[:, t, m],
+                    in_=w1_grouped[half][:, t].rearrange("p m j -> p (m j)"),
+                )
+
+        band_w_words = stage.tile([P, 2, N], I32, name="band_w_words", tag="staged", align_bytes=64)
+        nc.sync.dma_start(out=band_w_words[:, 0, :], in_=words_of(w2_words))
+        nc.sync.dma_start(out=band_w_words[:, 1, :], in_=words_of(w3_words))
+
+        hidden = {}
+        bands = {}
+        codes = {}
+        scales = {}
+
+        def first_layer(c, d):
+            acc = hidden_psum.tile([P, PACK, CHUNK], F32, name="acc")
+            cols = slice(c * CHUNK, (c + 1) * CHUNK)
+            scale_cols = slice(d * V + c * CHUNK, d * V + (c + 1) * CHUNK)
+            for t in range(PACK):
+                nc.tensor.matmul_mx(
+                    out=acc[:, t, :],
+                    lhsT=w1_codes[:, t, :].bitcast(FP8X4),
+                    lhsT_scale=w1_scales[:, t, :],
+                    rhs=picked_words[d][:, cols].bitcast(FP8X4),
+                    rhs_scale=picked_scales[:, scale_cols],
+                    start=True,
+                    stop=True,
+                )
+            hidden[c, d] = keep.tile([P, CHUNK, PACK], F32, name=f"hidden{c}_{d}")
+            nc.scalar.activation(hidden[c, d][:], acc[:].rearrange("p t v -> p v t"), ACT.Gelu_apprx_tanh)
+
+        def band(c, b):
+            bands[c, b] = keep.tile([P, CHUNK, PACK], BF16, name=f"band{c}_{b}", align_bytes=64)
+            nc.vector.tensor_tensor(bands[c, b][:], hidden[c, 0][:], hidden[c, 1][:], (ALU.add, ALU.subtract)[b])
+
+        def quantise(c, b):
+            codes[c, b] = keep.tile([P, CHUNK], U32, name=f"codes{c}_{b}", align_bytes=64)
+            scales[c, b] = keep.tile([P, CHUNK], U8, name=f"scales{c}_{b}", align_bytes=64)
+            nc.vector.quantize_mx(
+                out=codes[c, b][:].bitcast(FP8X4),
+                scales=scales[c, b][:],
+                in_=bands[c, b][:].rearrange("p v t -> p (v t)"),
+            )
+
+        def second_layer(c):
+            acc = out_psum.tile([N, CHUNK], F32, name="out_acc")
+            for b in range(2):
+                nc.tensor.matmul_mx(
+                    out=acc[:],
+                    lhsT=band_w_words[:, b, :].bitcast(FP8X4),
+                    lhsT_scale=band_w_scales[:, b * N : (b + 1) * N],
+                    rhs=codes[c, b][:].bitcast(FP8X4),
+                    rhs_scale=scales[c, b][:],
+                    start=(b == 0),
+                    stop=(b == 1),
+                )
+            result = keep.tile([N, CHUNK], F32, name=f"result{c}")
+            nc.scalar.activation(result[:], acc[:], ACT.Copy, scale=0.5)
+            queue = nc.scalar if c == chunks - 1 else nc.sync
+            queue.dma_start(out=out[:, c * CHUNK : (c + 1) * CHUNK], in_=result[:])
+
+        for c in range(chunks):
+            first_layer(c, 0)
+            first_layer(c, 1)
+        for c in range(chunks):
+            band(c, 0)
+            if c > 0:
+                quantise(c - 1, 1)
+            band(c, 1)
+            quantise(c, 0)
+            if c > 0:
+                second_layer(c - 1)
+        quantise(chunks - 1, 1)
+        second_layer(chunks - 1)

@@ -46,11 +46,15 @@ def tile_picked_haar_gelu_p_kernel(
         offsets = keep.tile([P, S // 16], U16, name="offsets")
         nc.sync.dma_start(offsets[:], offs)
 
-        table_scales = keep.tile([P, T], U8, name="table_scales", align_bytes=64)
+        table_scales = keep.tile([P, T], U8, name="table_scales", tag="scale_rows", align_bytes=64)
         nc.vector.memset(table_scales[:].bitcast(I32), 0)
+        warm = keep.tile([P, 2], F32, name="warm")
+        nc.gpsimd.memset(warm[:, 0:1], 0.0)
+        nc.scalar.activation(warm[:, 1:2], warm[:, 0:1], ACT.Gelu_apprx_tanh)
+
         table_words = keep.tile([P, T], I32, name="table_words", align_bytes=64)
         nc.sync.dma_start(out=table_words[:, :FIRST_WORDS], in_=words_of(x_words)[:, :FIRST_WORDS])
-        load_scale_rows(nc.sync, table_scales, x_scales[0])
+        nc.sync.dma_start(out=table_scales[0:P:8, :].bitcast(I32), in_=x_scales[0].bitcast(I32))
         nc.sync.dma_start(out=table_words[:, FIRST_WORDS:], in_=words_of(x_words)[:, FIRST_WORDS:])
 
         w1_rows = w1.rearrange("(p j) c -> p j c", j=PACK)
@@ -60,13 +64,17 @@ def tile_picked_haar_gelu_p_kernel(
             nc.sync.dma_start(out=raw[:], in_=w1_rows[:, :, half * (H // 2) : (half + 1) * (H // 2)])
             w1_raw.append(raw)
 
-        band_w_scales = keep.tile([P, 2 * N], U8, name="band_w_scales", align_bytes=64)
+        picked_scales = keep.tile([P, S], U8, name="picked_scales", align_bytes=64)
+        nc.vector.memset(picked_scales[:].bitcast(I32), 0)
+        picked_rows = keep.tile([P, S], U8, name="picked_rows", align_bytes=64)
+        nc.vector.tensor_copy(picked_rows[:], table_scales[:].indirect(offsets[:]))
+        load_scale_rows(nc.scalar, picked_scales, picked_rows[0:P:8, :])
+
+        band_w_scales = keep.tile([P, 2 * N], U8, name="band_w_scales", tag="scale_rows", align_bytes=64)
         nc.vector.memset(band_w_scales[:].bitcast(I32), 0)
         load_scale_rows(nc.sync, band_w_scales[:, 0:N], w2_scales[0])
         load_scale_rows(nc.sync, band_w_scales[:, N : 2 * N], w3_scales[0])
 
-        picked_scales = keep.tile([P, S], U8, name="picked_scales", align_bytes=64)
-        nc.vector.tensor_copy(picked_scales[:], table_scales[:].indirect(offsets[:]))
         picked_words = []
         for d in range(2):
             picked = keep.tile([P, V], U32, name=f"picked_words{d}", align_bytes=64)

@@ -19,8 +19,7 @@ P = 128
 PACK = 4
 CHUNK = 128
 HALF = P // 2
-VECTOR_SHARE = 44
-FIRST_WORDS = 1024
+HEAD = 32
 
 
 def load_scale_rows(queue, plane, rows):
@@ -39,10 +38,12 @@ def tile_picked_haar_gelu_p_kernel(
     chunks = V // CHUNK
     with ExitStack() as ctx:
         keep = ctx.enter_context(tc.tile_pool(name="keep", bufs=1))
-        stage = ctx.enter_context(tc.tile_pool(name="stage", bufs=2))
         hidden_psum = ctx.enter_context(tc.psum_pool(name="hidden_psum", bufs=6))
         out_psum = ctx.enter_context(tc.psum_pool(name="out_psum", bufs=2))
 
+        w1_rows = w1.rearrange("(p j) c -> p j c", j=PACK)
+        w1_upper = keep.tile([P, 2, H], F32, name="w1_upper", tag="staged", align_bytes=64)
+        nc.sync.dma_start(out=w1_upper[:], in_=w1_rows[:, :2])
         offsets = keep.tile([P, S // 16], U16, name="offsets")
         nc.sync.dma_start(offsets[:], offs)
 
@@ -53,16 +54,11 @@ def tile_picked_haar_gelu_p_kernel(
         nc.scalar.activation(warm[:, 1:2], warm[:, 0:1], ACT.Gelu_apprx_tanh)
 
         table_words = keep.tile([P, T], I32, name="table_words", align_bytes=64)
-        nc.sync.dma_start(out=table_words[:, :FIRST_WORDS], in_=words_of(x_words)[:, :FIRST_WORDS])
+        w1_lower = [keep.tile([P, 2, H // 2], F32, name=f"w1_lower{half}", align_bytes=64) for half in range(2)]
         nc.sync.dma_start(out=table_scales[0:P:8, :].bitcast(I32), in_=x_scales[0].bitcast(I32))
-        nc.sync.dma_start(out=table_words[:, FIRST_WORDS:], in_=words_of(x_words)[:, FIRST_WORDS:])
-
-        w1_rows = w1.rearrange("(p j) c -> p j c", j=PACK)
-        w1_raw = []
-        for half in range(2):
-            raw = stage.tile([P, PACK, H // 2], F32, name=f"w1_raw{half}", tag="staged", align_bytes=64)
-            nc.sync.dma_start(out=raw[:], in_=w1_rows[:, :, half * (H // 2) : (half + 1) * (H // 2)])
-            w1_raw.append(raw)
+        nc.sync.dma_start(out=w1_lower[0][:], in_=w1_rows[:, 2:, : H // 2])
+        nc.sync.dma_start(out=table_words[:], in_=words_of(x_words))
+        nc.sync.dma_start(out=w1_lower[1][:], in_=w1_rows[:, 2:, H // 2 :])
 
         picked_scales = keep.tile([P, S], U8, name="picked_scales", align_bytes=64)
         nc.vector.memset(picked_scales[:].bitcast(I32), 0)
@@ -75,27 +71,19 @@ def tile_picked_haar_gelu_p_kernel(
         load_scale_rows(nc.sync, band_w_scales[:, 0:N], w2_scales[0])
         load_scale_rows(nc.sync, band_w_scales[:, N : 2 * N], w3_scales[0])
 
-        picked_words = []
-        for d in range(2):
-            picked = keep.tile([P, V], U32, name=f"picked_words{d}", align_bytes=64)
-            piece = offsets[:, d * (V // 16) : (d + 1) * (V // 16)]
-            nc.vector.tensor_copy(picked[:], table_words[:].bitcast(U32).indirect(piece))
-            picked_words.append(picked)
+        w1_grouped = [
+            keep.tile([P, PACK, HALF, PACK], BF16, name=f"w1_grouped{half}", tag=f"grouped{half}", align_bytes=64)
+            for half in range(2)
+        ]
 
-        w1_grouped = [keep.tile([P, PACK, HALF, PACK], BF16, name=f"w1_grouped{half}", align_bytes=64) for half in range(2)]
-
-        def deal(copy, half, m0, m1):
-            src = w1_raw[half][:].rearrange("p j (m t) -> p m t j", t=PACK)[:, m0:m1]
-            dst = w1_grouped[half][:].rearrange("p t m j -> p m t j")[:, m0:m1]
-            copy(dst, src)
-
-        deal(nc.scalar.copy, 0, 0, HALF)
-        deal(nc.vector.tensor_copy, 1, 0, VECTOR_SHARE)
-        deal(nc.scalar.copy, 1, VECTOR_SHARE, HALF)
+        def deal(raw, half, slots):
+            dealt = w1_grouped[half][:].rearrange("p t m j -> p m t j")[:, :, :, slots]
+            nc.scalar.copy(dealt, raw.rearrange("p j (m t) -> p m t j", t=PACK))
 
         w1_codes = keep.tile([P, PACK, P], U32, name="w1_codes", align_bytes=64)
         w1_scales = keep.tile([P, PACK, P], U8, name="w1_scales", align_bytes=64)
-        for half in range(2):
+
+        def quantise_w1(half):
             m = slice(half * HALF, (half + 1) * HALF)
             for t in range(PACK):
                 nc.vector.quantize_mx(
@@ -104,7 +92,22 @@ def tile_picked_haar_gelu_p_kernel(
                     in_=w1_grouped[half][:, t].rearrange("p m j -> p (m j)"),
                 )
 
-        band_w_words = stage.tile([P, 2, N], I32, name="band_w_words", tag="staged", align_bytes=64)
+        def gather_words(picked, first, count):
+            entries = offsets[:, first // 16 : (first + count) // 16]
+            nc.vector.tensor_copy(picked[:], table_words[:].bitcast(U32).indirect(entries))
+
+        deal(w1_upper[:, :, : H // 2], 0, slice(0, 2))
+        deal(w1_lower[0][:], 0, slice(2, 4))
+        deal(w1_upper[:, :, H // 2 :], 1, slice(0, 2))
+        quantise_w1(0)
+        early_words = keep.tile([P, V + CHUNK], U32, name="early_words", align_bytes=64)
+        gather_words(early_words, 0, V + CHUNK)
+        deal(w1_lower[1][:], 1, slice(2, 4))
+        quantise_w1(1)
+        late_words = keep.tile([P, V], U32, name="late_words", tag="grouped1", align_bytes=64)
+        gather_words(late_words, V, V)
+
+        band_w_words = keep.tile([P, 2, N], I32, name="band_w_words", tag="staged", align_bytes=64)
         nc.sync.dma_start(out=band_w_words[:, 0, :], in_=words_of(w2_words))
         nc.sync.dma_start(out=band_w_words[:, 1, :], in_=words_of(w3_words))
 
@@ -113,26 +116,30 @@ def tile_picked_haar_gelu_p_kernel(
         codes = {}
         scales = {}
 
+        def parts(c):
+            return [slice(0, HEAD), slice(HEAD, CHUNK)] if c == 0 else [slice(0, CHUNK)]
+
         def first_layer(c, d):
             acc = hidden_psum.tile([P, PACK, CHUNK], F32, name="acc")
-            cols = slice(c * CHUNK, (c + 1) * CHUNK)
-            scale_cols = slice(d * V + c * CHUNK, d * V + (c + 1) * CHUNK)
+            first = d * V + c * CHUNK
+            scale_cols = slice(first, first + CHUNK)
+            words = early_words[:, scale_cols] if first < V + CHUNK else late_words[:, first - V : first - V + CHUNK]
             for t in range(PACK):
                 nc.tensor.matmul_mx(
                     out=acc[:, t, :],
                     lhsT=w1_codes[:, t, :].bitcast(FP8X4),
                     lhsT_scale=w1_scales[:, t, :],
-                    rhs=picked_words[d][:, cols].bitcast(FP8X4),
+                    rhs=words.bitcast(FP8X4),
                     rhs_scale=picked_scales[:, scale_cols],
                     start=True,
                     stop=True,
                 )
             hidden[c, d] = keep.tile([P, CHUNK, PACK], F32, name=f"hidden{c}_{d}")
-            nc.scalar.activation(hidden[c, d][:], acc[:].rearrange("p t v -> p v t"), ACT.Gelu_apprx_tanh)
+            for v in parts(c) if d == 1 else [slice(0, CHUNK)]:
+                nc.scalar.activation(hidden[c, d][:, v], acc[:].rearrange("p t v -> p v t")[:, v], ACT.Gelu_apprx_tanh)
 
-        def band(c, b):
-            bands[c, b] = keep.tile([P, CHUNK, PACK], BF16, name=f"band{c}_{b}", align_bytes=64)
-            nc.vector.tensor_tensor(bands[c, b][:], hidden[c, 0][:], hidden[c, 1][:], (ALU.add, ALU.subtract)[b])
+        def band(c, b, v):
+            nc.vector.tensor_tensor(bands[c, b][:, v], hidden[c, 0][:, v], hidden[c, 1][:, v], (ALU.add, ALU.subtract)[b])
 
         def quantise(c, b):
             codes[c, b] = keep.tile([P, CHUNK], U32, name=f"codes{c}_{b}", align_bytes=64)
@@ -164,10 +171,13 @@ def tile_picked_haar_gelu_p_kernel(
             first_layer(c, 0)
             first_layer(c, 1)
         for c in range(chunks):
-            band(c, 0)
-            if c > 0:
-                quantise(c - 1, 1)
-            band(c, 1)
+            for b in range(2):
+                bands[c, b] = keep.tile([P, CHUNK, PACK], BF16, name=f"band{c}_{b}", align_bytes=64)
+            for v in parts(c):
+                band(c, 0, v)
+                if c > 0:
+                    quantise(c - 1, 1)
+                band(c, 1, v)
             quantise(c, 0)
             if c > 0:
                 second_layer(c - 1)

@@ -17,9 +17,11 @@ ALU = mybir.AluOpType
 
 P = 128
 PACK = 4
-CHUNK = 128
-HALF = P // 2
+RUN = 64
+GROUP = 128
 HEAD = 32
+STEPS = [32, 32, 64, 64, 64, 128, 64, 64]
+PIECES = [(0, 32), (32, 64), (64, 96), (96, 128)]
 
 
 def load_scale_rows(queue, plane, rows):
@@ -35,81 +37,81 @@ def tile_picked_haar_gelu_p_kernel(
     tc, x_words, x_scales, w1, w2_words, w2_scales, w3_words, w3_scales, offs, out
 ):
     nc = tc.nc
-    chunks = V // CHUNK
+    runs = V // RUN
+    groups = V // GROUP
     with ExitStack() as ctx:
         keep = ctx.enter_context(tc.tile_pool(name="keep", bufs=1))
         hidden_psum = ctx.enter_context(tc.psum_pool(name="hidden_psum", bufs=6))
         out_psum = ctx.enter_context(tc.psum_pool(name="out_psum", bufs=2))
 
         w1_rows = w1.rearrange("(p j) c -> p j c", j=PACK)
-        w1_upper = keep.tile([P, 2, H], F32, name="w1_upper", tag="staged", align_bytes=64)
-        nc.sync.dma_start(out=w1_upper[:], in_=w1_rows[:, :2])
+        w1_raw = []
+        for lo, hi in PIECES:
+            w1_raw.append(keep.tile([P, PACK, PACK * (hi - lo)], F32, name=f"w1_raw{lo}", align_bytes=64))
+
+        def load_w1(i):
+            lo, hi = PIECES[i]
+            nc.sync.dma_start(out=w1_raw[i][:], in_=w1_rows[:, :, PACK * lo : PACK * hi])
+
+        for j in (slice(0, 2), slice(2, 4)):
+            nc.sync.dma_start(out=w1_raw[0][:, j], in_=w1_rows[:, j, : PACK * PIECES[0][1]])
         offsets = keep.tile([P, S // 16], U16, name="offsets")
         nc.sync.dma_start(offsets[:], offs)
 
         table_scales = keep.tile([P, T], U8, name="table_scales", tag="scale_rows", align_bytes=64)
-        nc.vector.memset(table_scales[:].bitcast(I32), 0)
-        warm = keep.tile([P, 2], F32, name="warm")
-        nc.gpsimd.memset(warm[:, 0:1], 0.0)
-        nc.scalar.activation(warm[:, 1:2], warm[:, 0:1], ACT.Gelu_apprx_tanh)
-
+        nc.vector.memset(table_scales[:, : T // 2].bitcast(I32), 0)
+        nc.gpsimd.memset(table_scales[:, T // 2 :].bitcast(I32), 0)
+        nc.sync.dma_start(out=table_scales[32:96:4, :].bitcast(I32), in_=x_scales[0].bitcast(I32))
         table_words = keep.tile([P, T], I32, name="table_words", align_bytes=64)
-        w1_lower = [keep.tile([P, 2, H // 2], F32, name=f"w1_lower{half}", align_bytes=64) for half in range(2)]
-        nc.sync.dma_start(out=table_scales[0:P:8, :].bitcast(I32), in_=x_scales[0].bitcast(I32))
-        nc.sync.dma_start(out=w1_lower[0][:], in_=w1_rows[:, 2:, : H // 2])
         nc.sync.dma_start(out=table_words[:], in_=words_of(x_words))
-        nc.sync.dma_start(out=w1_lower[1][:], in_=w1_rows[:, 2:, H // 2 :])
+        for i in range(1, len(PIECES)):
+            load_w1(i)
+
+        warm = keep.tile([P, 1], F32, name="warm")
+        nc.scalar.activation(warm[:], w1_raw[0][:, 0, 0:1], ACT.Gelu_apprx_tanh)
 
         picked_scales = keep.tile([P, S], U8, name="picked_scales", align_bytes=64)
         nc.vector.memset(picked_scales[:].bitcast(I32), 0)
         picked_rows = keep.tile([P, S], U8, name="picked_rows", align_bytes=64)
         nc.vector.tensor_copy(picked_rows[:], table_scales[:].indirect(offsets[:]))
-        load_scale_rows(nc.scalar, picked_scales, picked_rows[0:P:8, :])
+        paired_rows = keep.tile([P, S], U8, name="paired_rows", align_bytes=64)
+        nc.vector.tensor_copy(
+            paired_rows[:].bitcast(I32).rearrange("p (c d w) -> p c d w", d=2, c=runs),
+            picked_rows[:].bitcast(I32).rearrange("p (d c w) -> p c d w", d=2, c=runs),
+        )
+        load_scale_rows(nc.scalar, picked_scales, paired_rows[32:96:4, :])
+
+        w1_grouped = keep.tile([P, PACK, P, PACK], BF16, name="w1_grouped", align_bytes=64)
+
+        def deal(engine_copy, i, first, last):
+            lo, hi = PIECES[i]
+            dealt = w1_grouped[:, :, lo + first : lo + last, :].rearrange("p t m j -> p m j t")
+            engine_copy(dealt, w1_raw[i][:, :, PACK * first : PACK * last].rearrange("p j (m t) -> p m j t", t=PACK))
+
+        picked_words = keep.tile([P, S], U32, name="picked_words", align_bytes=64)
+        nc.vector.tensor_copy(
+            picked_words[:].rearrange("p (c d v) -> p d c v", d=2, c=runs),
+            table_words[:].bitcast(U32).indirect(offsets[:]),
+        )
+        for i, (lo, hi) in enumerate(PIECES):
+            deal(nc.scalar.copy, i, 0, hi - lo)
+
+        w1_codes = [keep.tile([P, P], U32, name=f"w1_codes{t}", align_bytes=64) for t in range(PACK)]
+        w1_scales = [keep.tile([P, P], U8, name=f"w1_scales{t}", align_bytes=64) for t in range(PACK)]
+        for t in range(PACK):
+            nc.vector.quantize_mx(
+                out=w1_codes[t][:].bitcast(FP8X4),
+                scales=w1_scales[t][:],
+                in_=w1_grouped[:, t].rearrange("p m j -> p (m j)"),
+            )
 
         band_w_scales = keep.tile([P, 2 * N], U8, name="band_w_scales", tag="scale_rows", align_bytes=64)
         nc.vector.memset(band_w_scales[:].bitcast(I32), 0)
-        load_scale_rows(nc.sync, band_w_scales[:, 0:N], w2_scales[0])
-        load_scale_rows(nc.sync, band_w_scales[:, N : 2 * N], w3_scales[0])
-
-        w1_grouped = [
-            keep.tile([P, PACK, HALF, PACK], BF16, name=f"w1_grouped{half}", tag=f"grouped{half}", align_bytes=64)
-            for half in range(2)
-        ]
-
-        def deal(raw, half, slots):
-            dealt = w1_grouped[half][:].rearrange("p t m j -> p m t j")[:, :, :, slots]
-            nc.scalar.copy(dealt, raw.rearrange("p j (m t) -> p m t j", t=PACK))
-
-        w1_codes = keep.tile([P, PACK, P], U32, name="w1_codes", align_bytes=64)
-        w1_scales = keep.tile([P, PACK, P], U8, name="w1_scales", align_bytes=64)
-
-        def quantise_w1(half):
-            m = slice(half * HALF, (half + 1) * HALF)
-            for t in range(PACK):
-                nc.vector.quantize_mx(
-                    out=w1_codes[:, t, m].bitcast(FP8X4),
-                    scales=w1_scales[:, t, m],
-                    in_=w1_grouped[half][:, t].rearrange("p m j -> p (m j)"),
-                )
-
-        def gather_words(picked, first, count):
-            entries = offsets[:, first // 16 : (first + count) // 16]
-            nc.vector.tensor_copy(picked[:], table_words[:].bitcast(U32).indirect(entries))
-
-        deal(w1_upper[:, :, : H // 2], 0, slice(0, 2))
-        deal(w1_lower[0][:], 0, slice(2, 4))
-        deal(w1_upper[:, :, H // 2 :], 1, slice(0, 2))
-        quantise_w1(0)
-        early_words = keep.tile([P, V + CHUNK], U32, name="early_words", align_bytes=64)
-        gather_words(early_words, 0, V + CHUNK)
-        deal(w1_lower[1][:], 1, slice(2, 4))
-        quantise_w1(1)
-        late_words = keep.tile([P, V], U32, name="late_words", tag="grouped1", align_bytes=64)
-        gather_words(late_words, V, V)
-
-        band_w_words = keep.tile([P, 2, N], I32, name="band_w_words", tag="staged", align_bytes=64)
+        band_w_words = keep.tile([P, 2, N], I32, name="band_w_words", align_bytes=64)
         nc.sync.dma_start(out=band_w_words[:, 0, :], in_=words_of(w2_words))
         nc.sync.dma_start(out=band_w_words[:, 1, :], in_=words_of(w3_words))
+        load_scale_rows(nc.sync, band_w_scales[:, 0:N], w2_scales[0])
+        load_scale_rows(nc.sync, band_w_scales[:, N : 2 * N], w3_scales[0])
 
         hidden = {}
         bands = {}
@@ -117,69 +119,75 @@ def tile_picked_haar_gelu_p_kernel(
         scales = {}
 
         def parts(c):
-            return [slice(0, HEAD), slice(HEAD, CHUNK)] if c == 0 else [slice(0, CHUNK)]
+            return [slice(0, HEAD), slice(HEAD, RUN)] if c == 0 else [slice(0, RUN)]
 
-        def first_layer(c, d):
-            acc = hidden_psum.tile([P, PACK, CHUNK], F32, name="acc")
-            first = d * V + c * CHUNK
-            scale_cols = slice(first, first + CHUNK)
-            words = early_words[:, scale_cols] if first < V + CHUNK else late_words[:, first - V : first - V + CHUNK]
+        def first_layer(c):
+            acc = hidden_psum.tile([P, PACK, 2 * RUN], F32, name="acc")
+            cols = slice(2 * RUN * c, 2 * RUN * (c + 1))
             for t in range(PACK):
                 nc.tensor.matmul_mx(
                     out=acc[:, t, :],
-                    lhsT=w1_codes[:, t, :].bitcast(FP8X4),
-                    lhsT_scale=w1_scales[:, t, :],
-                    rhs=words.bitcast(FP8X4),
-                    rhs_scale=picked_scales[:, scale_cols],
+                    lhsT=w1_codes[t][:].bitcast(FP8X4),
+                    lhsT_scale=w1_scales[t][:],
+                    rhs=picked_words[:, cols].bitcast(FP8X4),
+                    rhs_scale=picked_scales[:, cols],
                     start=True,
                     stop=True,
                 )
-            hidden[c, d] = keep.tile([P, CHUNK, PACK], F32, name=f"hidden{c}_{d}")
-            for v in parts(c) if d == 1 else [slice(0, CHUNK)]:
-                nc.scalar.activation(hidden[c, d][:, v], acc[:].rearrange("p t v -> p v t")[:, v], ACT.Gelu_apprx_tanh)
+            g, first = divmod(c * RUN, GROUP)
+            if g not in hidden:
+                hidden[g] = keep.tile([P, 2, GROUP, PACK], F32, name=f"hidden{g}")
+            for v in parts(c):
+                nc.scalar.activation(
+                    hidden[g][:, :, first + v.start : first + v.stop],
+                    acc[:].rearrange("p t (d v) -> p d v t", d=2)[:, :, v],
+                    ACT.Gelu_apprx_tanh,
+                )
 
-        def band(c, b, v):
-            nc.vector.tensor_tensor(bands[c, b][:, v], hidden[c, 0][:, v], hidden[c, 1][:, v], (ALU.add, ALU.subtract)[b])
+        def band(g, b, v):
+            if (g, b) not in bands:
+                bands[g, b] = keep.tile([P, GROUP, PACK], BF16, name=f"band{g}_{b}", align_bytes=64)
+            nc.vector.tensor_tensor(bands[g, b][:, v], hidden[g][:, 0, v], hidden[g][:, 1, v], (ALU.add, ALU.subtract)[b])
 
-        def quantise(c, b):
-            codes[c, b] = keep.tile([P, CHUNK], U32, name=f"codes{c}_{b}", align_bytes=64)
-            scales[c, b] = keep.tile([P, CHUNK], U8, name=f"scales{c}_{b}", align_bytes=64)
+        def quantise(g, b):
+            codes[g, b] = keep.tile([P, GROUP], U32, name=f"codes{g}_{b}", align_bytes=64)
+            scales[g, b] = keep.tile([P, GROUP], U8, name=f"scales{g}_{b}", align_bytes=64)
             nc.vector.quantize_mx(
-                out=codes[c, b][:].bitcast(FP8X4),
-                scales=scales[c, b][:],
-                in_=bands[c, b][:].rearrange("p v t -> p (v t)"),
+                out=codes[g, b][:].bitcast(FP8X4),
+                scales=scales[g, b][:],
+                in_=bands[g, b][:].rearrange("p v t -> p (v t)"),
             )
 
-        def second_layer(c):
-            acc = out_psum.tile([N, CHUNK], F32, name="out_acc")
+        def second_layer(g):
+            acc = out_psum.tile([N, GROUP], F32, name="out_acc")
             for b in range(2):
                 nc.tensor.matmul_mx(
                     out=acc[:],
                     lhsT=band_w_words[:, b, :].bitcast(FP8X4),
                     lhsT_scale=band_w_scales[:, b * N : (b + 1) * N],
-                    rhs=codes[c, b][:].bitcast(FP8X4),
-                    rhs_scale=scales[c, b][:],
+                    rhs=codes[g, b][:].bitcast(FP8X4),
+                    rhs_scale=scales[g, b][:],
                     start=(b == 0),
                     stop=(b == 1),
                 )
-            result = keep.tile([N, CHUNK], F32, name=f"result{c}")
+            result = keep.tile([N, GROUP], F32, name=f"result{g}")
             nc.scalar.activation(result[:], acc[:], ACT.Copy, scale=0.5)
-            queue = nc.scalar if c == chunks - 1 else nc.sync
-            queue.dma_start(out=out[:, c * CHUNK : (c + 1) * CHUNK], in_=result[:])
+            queue = nc.scalar if g == groups - 1 else nc.sync
+            queue.dma_start(out=out[:, g * GROUP : (g + 1) * GROUP], in_=result[:])
 
-        for c in range(chunks):
-            first_layer(c, 0)
-            first_layer(c, 1)
-        for c in range(chunks):
-            for b in range(2):
-                bands[c, b] = keep.tile([P, CHUNK, PACK], BF16, name=f"band{c}_{b}", align_bytes=64)
-            for v in parts(c):
-                band(c, 0, v)
-                if c > 0:
-                    quantise(c - 1, 1)
-                band(c, 1, v)
-            quantise(c, 0)
-            if c > 0:
-                second_layer(c - 1)
-        quantise(chunks - 1, 1)
-        second_layer(chunks - 1)
+        for c in range(runs):
+            first_layer(c)
+        done = 0
+        for step in STEPS:
+            g, first = divmod(done, GROUP)
+            v = slice(first, first + step)
+            band(g, 0, v)
+            if g > 0 and first == 0:
+                quantise(g - 1, 1)
+                second_layer(g - 1)
+            band(g, 1, v)
+            if v.stop == GROUP:
+                quantise(g, 0)
+            done = done + step
+        quantise(groups - 1, 1)
+        second_layer(groups - 1)

@@ -85,8 +85,8 @@ def tile_picked_haar_gelu_p_kernel(
 
         def deal(engine_copy, i, first, last):
             lo, hi = PIECES[i]
-            dealt = w1_grouped[:, :, lo + first : lo + last, :].rearrange("p t m j -> p m j t")
-            engine_copy(dealt, w1_raw[i][:, :, PACK * first : PACK * last].rearrange("p j (m t) -> p m j t", t=PACK))
+            dealt = w1_grouped[:, :, lo + first : lo + last, :].rearrange("p t m j -> p m t j")
+            engine_copy(dealt, w1_raw[i][:, :, PACK * first : PACK * last].rearrange("p j (m t) -> p m t j", t=PACK))
 
         picked_words = keep.tile([P, S], U32, name="picked_words", align_bytes=64)
         nc.vector.tensor_copy(

@@ -20,8 +20,10 @@ PACK = 4
 RUN = 64
 GROUP = 128
 HEAD = 32
-STEPS = [32, 32, 64, 64, 64, 128, 64, 64]
-PIECES = [(0, 32), (32, 64), (64, 96), (96, 128)]
+EARLY = 1024
+WARM_WIDTHS = [512, 512, 256]
+SCALAR_SHARE = 80
+STEPS = [32, 32, 64, 64, 64, 64, 64, 64, 64]
 
 
 def load_scale_rows(queue, plane, rows):
@@ -37,117 +39,106 @@ def tile_picked_haar_gelu_p_kernel(
     tc, x_words, x_scales, w1, w2_words, w2_scales, w3_words, w3_scales, offs, out
 ):
     nc = tc.nc
-    runs = V // RUN
     groups = V // GROUP
     with ExitStack() as ctx:
         keep = ctx.enter_context(tc.tile_pool(name="keep", bufs=1))
         hidden_psum = ctx.enter_context(tc.psum_pool(name="hidden_psum", bufs=6))
         out_psum = ctx.enter_context(tc.psum_pool(name="out_psum", bufs=2))
 
-        w1_rows = w1.rearrange("(p j) c -> p j c", j=PACK)
-        w1_raw = []
-        for lo, hi in PIECES:
-            w1_raw.append(keep.tile([P, PACK, PACK * (hi - lo)], F32, name=f"w1_raw{lo}", align_bytes=64))
-
-        def load_w1(i):
-            lo, hi = PIECES[i]
-            nc.sync.dma_start(out=w1_raw[i][:], in_=w1_rows[:, :, PACK * lo : PACK * hi])
-
-        for j in (slice(0, 2), slice(2, 4)):
-            nc.sync.dma_start(out=w1_raw[0][:, j], in_=w1_rows[:, j, : PACK * PIECES[0][1]])
+        table_words = keep.tile([P, T], I32, name="table_words", align_bytes=64)
+        nc.sync.dma_start(out=table_words[:, :EARLY], in_=words_of(x_words)[:, :EARLY])
         offsets = keep.tile([P, S // 16], U16, name="offsets")
         nc.sync.dma_start(offsets[:], offs)
-
         table_scales = keep.tile([P, T], U8, name="table_scales", tag="scale_rows", align_bytes=64)
         nc.vector.memset(table_scales[:, : T // 2].bitcast(I32), 0)
         nc.gpsimd.memset(table_scales[:, T // 2 :].bitcast(I32), 0)
         nc.sync.dma_start(out=table_scales[32:96:4, :].bitcast(I32), in_=x_scales[0].bitcast(I32))
-        table_words = keep.tile([P, T], I32, name="table_words", align_bytes=64)
-        nc.sync.dma_start(out=table_words[:], in_=words_of(x_words))
-        for i in range(1, len(PIECES)):
-            load_w1(i)
-
-        warm = keep.tile([P, 1], F32, name="warm")
-        nc.scalar.activation(warm[:], w1_raw[0][:, 0, 0:1], ACT.Gelu_apprx_tanh)
+        w1_raw = keep.tile([P, PACK, H], F32, name="w1_raw", tag="staged", align_bytes=64)
+        nc.sync.dma_start(out=w1_raw[:], in_=w1.rearrange("(p j) c -> p j c", j=PACK))
+        nc.sync.dma_start(out=table_words[:, EARLY:], in_=words_of(x_words)[:, EARLY:])
 
         picked_scales = keep.tile([P, S], U8, name="picked_scales", align_bytes=64)
         nc.vector.memset(picked_scales[:].bitcast(I32), 0)
         picked_rows = keep.tile([P, S], U8, name="picked_rows", align_bytes=64)
         nc.vector.tensor_copy(picked_rows[:], table_scales[:].indirect(offsets[:]))
-        paired_rows = keep.tile([P, S], U8, name="paired_rows", align_bytes=64)
-        nc.vector.tensor_copy(
-            paired_rows[:].bitcast(I32).rearrange("p (c d w) -> p c d w", d=2, c=runs),
-            picked_rows[:].bitcast(I32).rearrange("p (d c w) -> p c d w", d=2, c=runs),
-        )
-        load_scale_rows(nc.scalar, picked_scales, paired_rows[32:96:4, :])
-
-        w1_grouped = keep.tile([P, PACK, P, PACK], BF16, name="w1_grouped", align_bytes=64)
-
-        def deal(engine_copy, i, first, last):
-            lo, hi = PIECES[i]
-            dealt = w1_grouped[:, :, lo + first : lo + last, :].rearrange("p t m j -> p m t j")
-            engine_copy(dealt, w1_raw[i][:, :, PACK * first : PACK * last].rearrange("p j (m t) -> p m t j", t=PACK))
-
-        picked_words = keep.tile([P, S], U32, name="picked_words", align_bytes=64)
-        nc.vector.tensor_copy(
-            picked_words[:].rearrange("p (c d v) -> p d c v", d=2, c=runs),
-            table_words[:].bitcast(U32).indirect(offsets[:]),
-        )
-        for i, (lo, hi) in enumerate(PIECES):
-            deal(nc.scalar.copy, i, 0, hi - lo)
-
-        w1_codes = [keep.tile([P, P], U32, name=f"w1_codes{t}", align_bytes=64) for t in range(PACK)]
-        w1_scales = [keep.tile([P, P], U8, name=f"w1_scales{t}", align_bytes=64) for t in range(PACK)]
-        for t in range(PACK):
-            nc.vector.quantize_mx(
-                out=w1_codes[t][:].bitcast(FP8X4),
-                scales=w1_scales[t][:],
-                in_=w1_grouped[:, t].rearrange("p m j -> p (m j)"),
-            )
+        load_scale_rows(nc.sync, picked_scales, picked_rows[32:96:4, :])
 
         band_w_scales = keep.tile([P, 2 * N], U8, name="band_w_scales", tag="scale_rows", align_bytes=64)
         nc.vector.memset(band_w_scales[:].bitcast(I32), 0)
-        band_w_words = keep.tile([P, 2, N], I32, name="band_w_words", align_bytes=64)
-        nc.sync.dma_start(out=band_w_words[:, 0, :], in_=words_of(w2_words))
-        nc.sync.dma_start(out=band_w_words[:, 1, :], in_=words_of(w3_words))
         load_scale_rows(nc.sync, band_w_scales[:, 0:N], w2_scales[0])
         load_scale_rows(nc.sync, band_w_scales[:, N : 2 * N], w3_scales[0])
 
-        hidden = {}
+        w1_grouped = keep.tile([P, PACK, P, PACK], BF16, name="w1_grouped", align_bytes=64)
+        for engine_copy, m in ((nc.scalar.copy, slice(0, SCALAR_SHARE)), (nc.vector.tensor_copy, slice(SCALAR_SHARE, P))):
+            engine_copy(
+                w1_grouped[:].rearrange("p t m j -> p m t j")[:, m],
+                w1_raw[:].rearrange("p j (m t) -> p m t j", t=PACK)[:, m],
+            )
+        w1_codes = keep.tile([P, PACK * P], U32, name="w1_codes", align_bytes=64)
+        w1_scales = keep.tile([P, PACK * P], U8, name="w1_scales", align_bytes=64)
+        nc.vector.quantize_mx(
+            out=w1_codes[:].bitcast(FP8X4),
+            scales=w1_scales[:],
+            in_=w1_grouped[:].rearrange("p t m j -> p (t m j)"),
+        )
+
+        for width in WARM_WIDTHS:
+            idle = out_psum.tile([N, width], F32, name="out_acc")
+            nc.tensor.matmul_mx(
+                out=idle[:],
+                lhsT=w1_codes[:, :P].bitcast(FP8X4),
+                lhsT_scale=w1_scales[:, :P],
+                rhs=w1_codes[:, :width].bitcast(FP8X4),
+                rhs_scale=w1_scales[:, :width],
+                start=True,
+                stop=True,
+            )
+
+        band_w_words = keep.tile([P, 2, N], I32, name="band_w_words", tag="staged", align_bytes=64)
+        nc.sync.dma_start(out=band_w_words[:, 0, :], in_=words_of(w2_words))
+        nc.sync.dma_start(out=band_w_words[:, 1, :], in_=words_of(w3_words))
+
+        early_words = keep.tile([P, V + GROUP], U32, name="early_words", align_bytes=64)
+        late_words = keep.tile([P, V], U32, name="late_words", align_bytes=64)
+        for picked, first, count in ((early_words, 0, V + GROUP), (late_words, V, V)):
+            entries = offsets[:, first // 16 : (first + count) // 16]
+            nc.vector.tensor_copy(picked[:], table_words[:].bitcast(U32).indirect(entries))
+
+        hidden = keep.tile([P, 2, V, PACK], F32, name="hidden")
         bands = {}
         codes = {}
         scales = {}
 
-        def parts(c):
-            return [slice(0, HEAD), slice(HEAD, RUN)] if c == 0 else [slice(0, RUN)]
+        banks = {}
 
-        def first_layer(c):
-            acc = hidden_psum.tile([P, PACK, 2 * RUN], F32, name="acc")
-            cols = slice(2 * RUN * c, 2 * RUN * (c + 1))
+        def first_layer(d, first, count):
+            acc = hidden_psum.tile([P, PACK, count], F32, name="acc")
+            entry = d * V + first
+            words = early_words[:, entry : entry + count] if entry < V + GROUP else late_words[:, first : first + count]
             for t in range(PACK):
                 nc.tensor.matmul_mx(
-                    out=acc[:, t, :],
-                    lhsT=w1_codes[t][:].bitcast(FP8X4),
-                    lhsT_scale=w1_scales[t][:],
-                    rhs=picked_words[:, cols].bitcast(FP8X4),
-                    rhs_scale=picked_scales[:, cols],
+                    out=acc[:, t],
+                    lhsT=w1_codes[:, t * P : (t + 1) * P].bitcast(FP8X4),
+                    lhsT_scale=w1_scales[:, t * P : (t + 1) * P],
+                    rhs=words.bitcast(FP8X4),
+                    rhs_scale=picked_scales[:, entry : entry + count],
                     start=True,
                     stop=True,
                 )
-            g, first = divmod(c * RUN, GROUP)
-            if g not in hidden:
-                hidden[g] = keep.tile([P, 2, GROUP, PACK], F32, name=f"hidden{g}")
-            for v in parts(c):
-                nc.scalar.activation(
-                    hidden[g][:, :, first + v.start : first + v.stop],
-                    acc[:].rearrange("p t (d v) -> p d v t", d=2)[:, :, v],
-                    ACT.Gelu_apprx_tanh,
-                )
+            for v in range(first, first + count):
+                banks[d, v] = (acc, first)
+
+        def gelu(d, lo, hi):
+            acc, first = banks[d, lo]
+            nc.scalar.activation(
+                hidden[:, d, lo:hi], acc[:].rearrange("p t v -> p v t")[:, lo - first : hi - first], ACT.Gelu_apprx_tanh
+            )
 
         def band(g, b, v):
             if (g, b) not in bands:
                 bands[g, b] = keep.tile([P, GROUP, PACK], BF16, name=f"band{g}_{b}", align_bytes=64)
-            nc.vector.tensor_tensor(bands[g, b][:, v], hidden[g][:, 0, v], hidden[g][:, 1, v], (ALU.add, ALU.subtract)[b])
+            pairs = slice(g * GROUP + v.start, g * GROUP + v.stop)
+            nc.vector.tensor_tensor(bands[g, b][:, v], hidden[:, 0, pairs], hidden[:, 1, pairs], (ALU.add, ALU.subtract)[b])
 
         def quantise(g, b):
             codes[g, b] = keep.tile([P, GROUP], U32, name=f"codes{g}_{b}", align_bytes=64)
@@ -175,8 +166,25 @@ def tile_picked_haar_gelu_p_kernel(
             queue = nc.scalar if g == groups - 1 else nc.sync
             queue.dma_start(out=out[:, g * GROUP : (g + 1) * GROUP], in_=result[:])
 
-        for c in range(runs):
-            first_layer(c)
+        first_layer(0, 0, RUN)
+        gelu(0, 0, RUN)
+        first_layer(1, 0, GROUP)
+        gelu(1, 0, HEAD)
+        gelu(1, HEAD, RUN)
+        first_layer(0, RUN, GROUP)
+        gelu(0, RUN, GROUP)
+        gelu(1, RUN, GROUP)
+        gelu(0, GROUP, GROUP + RUN)
+        first_layer(1, GROUP, GROUP)
+        gelu(1, GROUP, GROUP + RUN)
+        gelu(1, GROUP + RUN, 2 * GROUP)
+        for first in range(GROUP + RUN, V - RUN, GROUP):
+            first_layer(0, first, GROUP)
+            gelu(0, first, first + GROUP)
+            first_layer(1, first + RUN, GROUP)
+            gelu(1, first + RUN, first + RUN + GROUP)
+        first_layer(0, V - RUN, RUN)
+        gelu(0, V - RUN, V)
         done = 0
         for step in STEPS:
             g, first = divmod(done, GROUP)

@@ -20,9 +20,7 @@ PACK = 4
 RUN = 64
 GROUP = 128
 HEAD = 32
-EARLY = 1024
 WARM_WIDTHS = [512, 512, 256]
-SCALAR_SHARE = 80
 STEPS = [32, 32, 64, 64, 64, 64, 64, 64, 64]
 
 
@@ -45,17 +43,15 @@ def tile_picked_haar_gelu_p_kernel(
         hidden_psum = ctx.enter_context(tc.psum_pool(name="hidden_psum", bufs=6))
         out_psum = ctx.enter_context(tc.psum_pool(name="out_psum", bufs=2))
 
-        table_words = keep.tile([P, T], I32, name="table_words", align_bytes=64)
-        nc.sync.dma_start(out=table_words[:, :EARLY], in_=words_of(x_words)[:, :EARLY])
+        w1_raw = keep.tile([P, PACK, H], F32, name="w1_raw", tag="staged", align_bytes=64)
+        nc.sync.dma_start(out=w1_raw[:], in_=w1.rearrange("(p j) c -> p j c", j=PACK))
         offsets = keep.tile([P, S // 16], U16, name="offsets")
         nc.sync.dma_start(offsets[:], offs)
         table_scales = keep.tile([P, T], U8, name="table_scales", tag="scale_rows", align_bytes=64)
-        nc.vector.memset(table_scales[:, : T // 2].bitcast(I32), 0)
-        nc.gpsimd.memset(table_scales[:, T // 2 :].bitcast(I32), 0)
+        nc.vector.memset(table_scales[:].bitcast(I32), 0)
         nc.sync.dma_start(out=table_scales[32:96:4, :].bitcast(I32), in_=x_scales[0].bitcast(I32))
-        w1_raw = keep.tile([P, PACK, H], F32, name="w1_raw", tag="staged", align_bytes=64)
-        nc.sync.dma_start(out=w1_raw[:], in_=w1.rearrange("(p j) c -> p j c", j=PACK))
-        nc.sync.dma_start(out=table_words[:, EARLY:], in_=words_of(x_words)[:, EARLY:])
+        table_words = keep.tile([P, T], I32, name="table_words", align_bytes=64)
+        nc.sync.dma_start(out=table_words[:], in_=words_of(x_words))
 
         picked_scales = keep.tile([P, S], U8, name="picked_scales", align_bytes=64)
         nc.vector.memset(picked_scales[:].bitcast(I32), 0)
@@ -69,11 +65,9 @@ def tile_picked_haar_gelu_p_kernel(
         load_scale_rows(nc.sync, band_w_scales[:, N : 2 * N], w3_scales[0])
 
         w1_grouped = keep.tile([P, PACK, P, PACK], BF16, name="w1_grouped", align_bytes=64)
-        for engine_copy, m in ((nc.scalar.copy, slice(0, SCALAR_SHARE)), (nc.vector.tensor_copy, slice(SCALAR_SHARE, P))):
-            engine_copy(
-                w1_grouped[:].rearrange("p t m j -> p m t j")[:, m],
-                w1_raw[:].rearrange("p j (m t) -> p m t j", t=PACK)[:, m],
-            )
+        nc.scalar.copy(
+            w1_grouped[:].rearrange("p t m j -> p m t j"), w1_raw[:].rearrange("p j (m t) -> p m t j", t=PACK)
+        )
         w1_codes = keep.tile([P, PACK * P], U32, name="w1_codes", align_bytes=64)
         w1_scales = keep.tile([P, PACK * P], U8, name="w1_scales", align_bytes=64)
         nc.vector.quantize_mx(
@@ -105,9 +99,9 @@ def tile_picked_haar_gelu_p_kernel(
             nc.vector.tensor_copy(picked[:], table_words[:].bitcast(U32).indirect(entries))
 
         hidden = keep.tile([P, 2, V, PACK], F32, name="hidden")
-        bands = {}
-        codes = {}
-        scales = {}
+        bands = [keep.tile([P, 2, GROUP, PACK], BF16, name=f"bands{g}", align_bytes=64) for g in range(groups)]
+        codes = [keep.tile([P, 2, GROUP], U32, name=f"codes{g}", align_bytes=64) for g in range(groups)]
+        scales = [keep.tile([P, 2, GROUP], U8, name=f"scales{g}", align_bytes=64) for g in range(groups)]
 
         banks = {}
 
@@ -135,18 +129,14 @@ def tile_picked_haar_gelu_p_kernel(
             )
 
         def band(g, b, v):
-            if (g, b) not in bands:
-                bands[g, b] = keep.tile([P, GROUP, PACK], BF16, name=f"band{g}_{b}", align_bytes=64)
             pairs = slice(g * GROUP + v.start, g * GROUP + v.stop)
-            nc.vector.tensor_tensor(bands[g, b][:, v], hidden[:, 0, pairs], hidden[:, 1, pairs], (ALU.add, ALU.subtract)[b])
+            nc.vector.tensor_tensor(bands[g][:, b, v], hidden[:, 0, pairs], hidden[:, 1, pairs], (ALU.add, ALU.subtract)[b])
 
         def quantise(g, b):
-            codes[g, b] = keep.tile([P, GROUP], U32, name=f"codes{g}_{b}", align_bytes=64)
-            scales[g, b] = keep.tile([P, GROUP], U8, name=f"scales{g}_{b}", align_bytes=64)
             nc.vector.quantize_mx(
-                out=codes[g, b][:].bitcast(FP8X4),
-                scales=scales[g, b][:],
-                in_=bands[g, b][:].rearrange("p v t -> p (v t)"),
+                out=codes[g][:, b].rearrange("p b v -> p (b v)").bitcast(FP8X4),
+                scales=scales[g][:, b].rearrange("p b v -> p (b v)"),
+                in_=bands[g][:, b].rearrange("p b v t -> p (b v t)"),
             )
 
         def second_layer(g):
@@ -156,8 +146,8 @@ def tile_picked_haar_gelu_p_kernel(
                     out=acc[:],
                     lhsT=band_w_words[:, b, :].bitcast(FP8X4),
                     lhsT_scale=band_w_scales[:, b * N : (b + 1) * N],
-                    rhs=codes[g, b][:].bitcast(FP8X4),
-                    rhs_scale=scales[g, b][:],
+                    rhs=codes[g][:, b].bitcast(FP8X4),
+                    rhs_scale=scales[g][:, b],
                     start=(b == 0),
                     stop=(b == 1),
                 )
@@ -191,11 +181,10 @@ def tile_picked_haar_gelu_p_kernel(
             v = slice(first, first + step)
             band(g, 0, v)
             if g > 0 and first == 0:
-                quantise(g - 1, 1)
+                quantise(g - 1, slice(0, 2))
                 second_layer(g - 1)
             band(g, 1, v)
-            if v.stop == GROUP:
-                quantise(g, 0)
             done = done + step
-        quantise(groups - 1, 1)
+        quantise(groups - 1, slice(0, 1))
+        quantise(groups - 1, slice(1, 2))
         second_layer(groups - 1)

@@ -20,7 +20,8 @@ PACK = 4
 RUN = 64
 GROUP = 128
 HEAD = 32
-WARM_WIDTHS = [512, 512, 256]
+WARM_PASSES = 4
+WARM_COLUMNS = 64
 STEPS = [32, 32, 64, 64, 64, 64, 64, 64, 64]
 
 
@@ -76,14 +77,14 @@ def tile_picked_haar_gelu_p_kernel(
             in_=w1_grouped[:].rearrange("p t m j -> p (t m j)"),
         )
 
-        for width in WARM_WIDTHS:
-            idle = out_psum.tile([N, width], F32, name="out_acc")
+        for turn in range(WARM_PASSES):
+            idle = out_psum.tile([WARM_COLUMNS, H], F32, name="out_acc")
             nc.tensor.matmul_mx(
                 out=idle[:],
-                lhsT=w1_codes[:, :P].bitcast(FP8X4),
-                lhsT_scale=w1_scales[:, :P],
-                rhs=w1_codes[:, :width].bitcast(FP8X4),
-                rhs_scale=w1_scales[:, :width],
+                lhsT=w1_codes[:, :WARM_COLUMNS].bitcast(FP8X4),
+                lhsT_scale=w1_scales[:, :WARM_COLUMNS],
+                rhs=w1_codes[:].bitcast(FP8X4),
+                rhs_scale=w1_scales[:],
                 start=True,
                 stop=True,
             )
@@ -180,11 +181,15 @@ def tile_picked_haar_gelu_p_kernel(
             g, first = divmod(done, GROUP)
             v = slice(first, first + step)
             band(g, 0, v)
-            if g > 0 and first == 0:
+            if 0 < g < groups - 1 and first == 0:
                 quantise(g - 1, slice(0, 2))
                 second_layer(g - 1)
+            if g == groups - 1 and first == 0:
+                quantise(g - 1, slice(0, 1))
             band(g, 1, v)
             done = done + step
+        quantise(groups - 2, slice(1, 2))
+        second_layer(groups - 2)
         quantise(groups - 1, slice(0, 1))
         quantise(groups - 1, slice(1, 2))
         second_layer(groups - 1)

@@ -22,12 +22,12 @@ GROUP = 128
 HEAD = 32
 WARM_PASSES = 4
 WARM_COLUMNS = 64
-STEPS = [32, 32, 64, 64, 64, 64, 64, 64, 64]
+STEPS = [32, 32, 64, 64, 64, 64, 64, 128]
 
 
-def load_scale_rows(queue, plane, rows):
+def load_scale_rows(queues, plane, rows):
     for r in range(4):
-        queue.dma_start(out=plane[r:P:32, :].bitcast(I32), in_=rows[r:16:4, :].bitcast(I32))
+        queues[r % len(queues)].dma_start(out=plane[r:P:32, :].bitcast(I32), in_=rows[r:16:4, :].bitcast(I32))
 
 
 def words_of(packed):
@@ -58,12 +58,12 @@ def tile_picked_haar_gelu_p_kernel(
         nc.vector.memset(picked_scales[:].bitcast(I32), 0)
         picked_rows = keep.tile([P, S], U8, name="picked_rows", align_bytes=64)
         nc.vector.tensor_copy(picked_rows[:], table_scales[:].indirect(offsets[:]))
-        load_scale_rows(nc.sync, picked_scales, picked_rows[32:96:4, :])
+        load_scale_rows([nc.sync, nc.scalar], picked_scales, picked_rows[32:96:4, :])
 
         band_w_scales = keep.tile([P, 2 * N], U8, name="band_w_scales", tag="scale_rows", align_bytes=64)
         nc.vector.memset(band_w_scales[:].bitcast(I32), 0)
-        load_scale_rows(nc.sync, band_w_scales[:, 0:N], w2_scales[0])
-        load_scale_rows(nc.sync, band_w_scales[:, N : 2 * N], w3_scales[0])
+        load_scale_rows([nc.sync], band_w_scales[:, 0:N], w2_scales[0])
+        load_scale_rows([nc.sync], band_w_scales[:, N : 2 * N], w3_scales[0])
 
         w1_grouped = keep.tile([P, PACK, P, PACK], BF16, name="w1_grouped", align_bytes=64)
         nc.scalar.copy(

@@ -1,6 +1,7 @@
 from contextlib import ExitStack
 
 import concourse.mybir as mybir
+from concourse.masks import make_identity
 
 K, T, S, V, H, N = 512, 4096, 1024, 512, 512, 128
 FLOPS = 2 * K * H * S + 2 * 2 * H * N * V
@@ -20,9 +21,7 @@ PACK = 4
 RUN = 64
 GROUP = 128
 HEAD = 32
-WARM_PASSES = 4
-WARM_COLUMNS = 64
-STEPS = [32, 32, 64, 64, 64, 64, 64, 128]
+WARM_WIDTHS = (512, 512, 256)
 
 
 def load_scale_rows(queues, plane, rows):
@@ -38,11 +37,12 @@ def tile_picked_haar_gelu_p_kernel(
     tc, x_words, x_scales, w1, w2_words, w2_scales, w3_words, w3_scales, offs, out
 ):
     nc = tc.nc
-    groups = V // GROUP
     with ExitStack() as ctx:
         keep = ctx.enter_context(tc.tile_pool(name="keep", bufs=1))
-        hidden_psum = ctx.enter_context(tc.psum_pool(name="hidden_psum", bufs=6))
-        out_psum = ctx.enter_context(tc.psum_pool(name="out_psum", bufs=2))
+        psum = ctx.enter_context(tc.psum_pool(name="psum", bufs=1))
+
+        def bank(number, shape):
+            return psum.tile(shape, F32, name=f"bank{number}", tag=f"bank{number}")
 
         w1_raw = keep.tile([P, PACK, H], F32, name="w1_raw", tag="staged", align_bytes=64)
         nc.sync.dma_start(out=w1_raw[:], in_=w1.rearrange("(p j) c -> p j c", j=PACK))
@@ -65,6 +65,9 @@ def tile_picked_haar_gelu_p_kernel(
         load_scale_rows([nc.sync], band_w_scales[:, 0:N], w2_scales[0])
         load_scale_rows([nc.sync], band_w_scales[:, N : 2 * N], w3_scales[0])
 
+        identity = keep.tile([P, P], F32, name="identity", align_bytes=64)
+        make_identity(nc, identity[:])
+
         w1_grouped = keep.tile([P, PACK, P, PACK], BF16, name="w1_grouped", align_bytes=64)
         nc.scalar.copy(
             w1_grouped[:].rearrange("p t m j -> p m t j"), w1_raw[:].rearrange("p j (m t) -> p m t j", t=PACK)
@@ -77,14 +80,14 @@ def tile_picked_haar_gelu_p_kernel(
             in_=w1_grouped[:].rearrange("p t m j -> p (t m j)"),
         )
 
-        for turn in range(WARM_PASSES):
-            idle = out_psum.tile([WARM_COLUMNS, H], F32, name="out_acc")
+        for turn_number, width in enumerate(WARM_WIDTHS):
+            idle = bank(5 + turn_number, [P, H])
             nc.tensor.matmul_mx(
-                out=idle[:],
-                lhsT=w1_codes[:, :WARM_COLUMNS].bitcast(FP8X4),
-                lhsT_scale=w1_scales[:, :WARM_COLUMNS],
-                rhs=w1_codes[:].bitcast(FP8X4),
-                rhs_scale=w1_scales[:],
+                out=idle[:, :width],
+                lhsT=w1_codes[:, :P].bitcast(FP8X4),
+                lhsT_scale=w1_scales[:, :P],
+                rhs=w1_codes[:, :width].bitcast(FP8X4),
+                rhs_scale=w1_scales[:, :width],
                 start=True,
                 stop=True,
             )
@@ -100,22 +103,27 @@ def tile_picked_haar_gelu_p_kernel(
             nc.vector.tensor_copy(picked[:], table_words[:].bitcast(U32).indirect(entries))
 
         hidden = keep.tile([P, 2, V, PACK], F32, name="hidden")
-        bands = [keep.tile([P, 2, GROUP, PACK], BF16, name=f"bands{g}", align_bytes=64) for g in range(groups)]
-        codes = [keep.tile([P, 2, GROUP], U32, name=f"codes{g}", align_bytes=64) for g in range(groups)]
-        scales = [keep.tile([P, 2, GROUP], U8, name=f"scales{g}", align_bytes=64) for g in range(groups)]
+        stretches = {"first": (0, GROUP), "second": (GROUP, GROUP), "turned": (2 * GROUP, GROUP), "last": (3 * GROUP, GROUP)}
+        bands = {k: keep.tile([P, 2, n, PACK], BF16, name=f"bands_{k}", align_bytes=64) for k, (f, n) in stretches.items()}
+        codes = {k: keep.tile([P, 2, n], U32, name=f"codes_{k}", align_bytes=64) for k, (f, n) in stretches.items()}
+        scales = {k: keep.tile([P, 2, n], U8, name=f"scales_{k}", align_bytes=64) for k, (f, n) in stretches.items()}
 
         banks = {}
 
-        def first_layer(d, first, count):
-            acc = hidden_psum.tile([P, PACK, count], F32, name="acc")
+        def picked_words(entry, count):
+            if entry < V + GROUP:
+                return early_words[:, entry : entry + count].bitcast(FP8X4)
+            return late_words[:, entry - V : entry - V + count].bitcast(FP8X4)
+
+        def first_layer(d, first, count, number):
+            acc = bank(number, [P, PACK, count])
             entry = d * V + first
-            words = early_words[:, entry : entry + count] if entry < V + GROUP else late_words[:, first : first + count]
             for t in range(PACK):
                 nc.tensor.matmul_mx(
                     out=acc[:, t],
                     lhsT=w1_codes[:, t * P : (t + 1) * P].bitcast(FP8X4),
                     lhsT_scale=w1_scales[:, t * P : (t + 1) * P],
-                    rhs=words.bitcast(FP8X4),
+                    rhs=picked_words(entry, count),
                     rhs_scale=picked_scales[:, entry : entry + count],
                     start=True,
                     stop=True,
@@ -129,67 +137,117 @@ def tile_picked_haar_gelu_p_kernel(
                 hidden[:, d, lo:hi], acc[:].rearrange("p t v -> p v t")[:, lo - first : hi - first], ACT.Gelu_apprx_tanh
             )
 
-        def band(g, b, v):
-            pairs = slice(g * GROUP + v.start, g * GROUP + v.stop)
-            nc.vector.tensor_tensor(bands[g][:, b, v], hidden[:, 0, pairs], hidden[:, 1, pairs], (ALU.add, ALU.subtract)[b])
+        def first_layer_by_token(d, name, number):
+            acc = bank(number, [P, H])
+            entry = d * V + stretches["turned"][0]
+            nc.tensor.matmul_mx(
+                out=acc[:],
+                lhsT=picked_words(entry, GROUP),
+                lhsT_scale=picked_scales[:, entry : entry + GROUP],
+                rhs=w1_codes[:].bitcast(FP8X4),
+                rhs_scale=w1_scales[:],
+                start=True,
+                stop=True,
+            )
+            rows = keep.tile([P, PACK, P], F32, name=name, tag=name, align_bytes=64)
+            nc.scalar.activation(rows[:].rearrange("v t m -> v (t m)"), acc[:], ACT.Gelu_apprx_tanh)
+            return rows
 
-        def quantise(g, b):
+        def turn(acc, rows, opens):
+            for t in range(PACK):
+                nc.tensor.matmul(
+                    acc[:, t],
+                    rows[:, t],
+                    identity[:],
+                    is_transpose=True,
+                    start=(opens and t == 0),
+                    stop=(not opens and t == PACK - 1),
+                )
+
+        def sums(k, lo, hi):
+            first = stretches[k][0]
+            for b, op in enumerate((ALU.add, ALU.subtract)):
+                nc.vector.tensor_tensor(bands[k][:, b, lo - first : hi - first], hidden[:, 0, lo:hi], hidden[:, 1, lo:hi], op)
+
+        def quantise(k, b):
             nc.vector.quantize_mx(
-                out=codes[g][:, b].rearrange("p b v -> p (b v)").bitcast(FP8X4),
-                scales=scales[g][:, b].rearrange("p b v -> p (b v)"),
-                in_=bands[g][:, b].rearrange("p b v t -> p (b v t)"),
+                out=codes[k][:, b].rearrange("p b v -> p (b v)").bitcast(FP8X4),
+                scales=scales[k][:, b].rearrange("p b v -> p (b v)"),
+                in_=bands[k][:, b].rearrange("p b v t -> p (b v t)"),
             )
 
-        def second_layer(g):
-            acc = out_psum.tile([N, GROUP], F32, name="out_acc")
+        def second_layer(k, number):
+            acc = bank(number, [N, GROUP])
             for b in range(2):
                 nc.tensor.matmul_mx(
                     out=acc[:],
                     lhsT=band_w_words[:, b, :].bitcast(FP8X4),
                     lhsT_scale=band_w_scales[:, b * N : (b + 1) * N],
-                    rhs=codes[g][:, b].bitcast(FP8X4),
-                    rhs_scale=scales[g][:, b],
+                    rhs=codes[k][:, b].bitcast(FP8X4),
+                    rhs_scale=scales[k][:, b],
                     start=(b == 0),
                     stop=(b == 1),
                 )
-            result = keep.tile([N, GROUP], F32, name=f"result{g}")
-            nc.scalar.activation(result[:], acc[:], ACT.Copy, scale=0.5)
-            queue = nc.scalar if g == groups - 1 else nc.sync
-            queue.dma_start(out=out[:, g * GROUP : (g + 1) * GROUP], in_=result[:])
+            return acc
 
-        first_layer(0, 0, RUN)
+        def store(k, acc, queue):
+            first, count = stretches[k]
+            tag = "first_rows" if k == "second" else f"result_{k}"
+            result = keep.tile([N, count], F32, name=f"result_{k}", tag=tag, align_bytes=64)
+            nc.scalar.activation(result[:], acc[:], ACT.Copy, scale=0.5)
+            queue.dma_start(out=out[:, first : first + count], in_=result[:])
+
+        low, high, both = slice(0, 1), slice(1, 2), slice(0, 2)
+        first_layer(0, 0, RUN, 0)
         gelu(0, 0, RUN)
-        first_layer(1, 0, GROUP)
+        first_layer(1, 0, GROUP, 1)
         gelu(1, 0, HEAD)
+        sums("first", 0, HEAD)
         gelu(1, HEAD, RUN)
-        first_layer(0, RUN, GROUP)
+        sums("first", HEAD, RUN)
+        first_layer(0, RUN, GROUP, 2)
         gelu(0, RUN, GROUP)
         gelu(1, RUN, GROUP)
+        sums("first", RUN, GROUP)
         gelu(0, GROUP, GROUP + RUN)
-        first_layer(1, GROUP, GROUP)
+        first_layer(1, GROUP, GROUP, 3)
         gelu(1, GROUP, GROUP + RUN)
+        sums("second", GROUP, GROUP + RUN)
+        quantise("first", both)
+        first_layer(0, GROUP + RUN, RUN, 4)
+        gelu(0, GROUP + RUN, 2 * GROUP)
         gelu(1, GROUP + RUN, 2 * GROUP)
-        for first in range(GROUP + RUN, V - RUN, GROUP):
-            first_layer(0, first, GROUP)
-            gelu(0, first, first + GROUP)
-            first_layer(1, first + RUN, GROUP)
-            gelu(1, first + RUN, first + RUN + GROUP)
-        first_layer(0, V - RUN, RUN)
-        gelu(0, V - RUN, V)
-        done = 0
-        for step in STEPS:
-            g, first = divmod(done, GROUP)
-            v = slice(first, first + step)
-            band(g, 0, v)
-            if 0 < g < groups - 1 and first == 0:
-                quantise(g - 1, slice(0, 2))
-                second_layer(g - 1)
-            if g == groups - 1 and first == 0:
-                quantise(g - 1, slice(0, 1))
-            band(g, 1, v)
-            done = done + step
-        quantise(groups - 2, slice(1, 2))
-        second_layer(groups - 2)
-        quantise(groups - 1, slice(0, 1))
-        quantise(groups - 1, slice(1, 2))
-        second_layer(groups - 1)
+        sums("second", GROUP + RUN, 2 * GROUP)
+
+        first_acc = second_layer("first", 3)
+        second_rows = first_layer_by_token(1, "second_rows", 5)
+        first_rows = first_layer_by_token(0, "first_rows", 6)
+        last = stretches["last"][0]
+        first_layer(0, last, GROUP, 7)
+        first_layer(1, last, GROUP, 0)
+        negated_rows = keep.tile([P, PACK, P], F32, name="negated_rows", align_bytes=64)
+        nc.vector.tensor_scalar(negated_rows[:], second_rows[:], -1.0, None, ALU.mult)
+        quantise("second", both)
+        low_acc = bank(1, [P, PACK, GROUP])
+        high_acc = bank(2, [P, PACK, GROUP])
+        turn(low_acc, second_rows, True)
+        turn(low_acc, first_rows, False)
+        turn(high_acc, negated_rows, True)
+        turn(high_acc, first_rows, False)
+        second_acc = second_layer("second", 4)
+        store("first", first_acc, nc.sync)
+        for lo in range(last, V, RUN):
+            gelu(0, lo, lo + RUN)
+            gelu(1, lo, lo + RUN)
+            sums("last", lo, lo + RUN)
+        for b, acc in enumerate((low_acc, high_acc)):
+            nc.scalar.activation(bands["turned"][:, b], acc[:].rearrange("p t v -> p v t"), ACT.Copy)
+        quantise("last", low)
+        quantise("last", high)
+        last_acc = second_layer("last", 5)
+        quantise("turned", low)
+        quantise("turned", high)
+        store("second", second_acc, nc.sync)
+        turned_acc = second_layer("turned", 6)
+        store("last", last_acc, nc.sync)
+        store("turned", turned_acc, nc.scalar)

@@ -192,12 +192,13 @@ def tile_picked_haar_gelu_p_kernel(
 
         def store(k, acc, queue):
             first, count = stretches[k]
-            tag = "first_rows" if k == "second" else f"result_{k}"
+            tag = {"first": "first_rows", "second": "negated_rows"}.get(k, f"result_{k}")
             result = keep.tile([N, count], F32, name=f"result_{k}", tag=tag, align_bytes=64)
             nc.scalar.activation(result[:], acc[:], ACT.Copy, scale=0.5)
             queue.dma_start(out=out[:, first : first + count], in_=result[:])
 
         low, high, both = slice(0, 1), slice(1, 2), slice(0, 2)
+        last = stretches["last"][0]
         first_layer(0, 0, RUN, 0)
         gelu(0, 0, RUN)
         first_layer(1, 0, GROUP, 1)
@@ -214,28 +215,25 @@ def tile_picked_haar_gelu_p_kernel(
         gelu(1, GROUP, GROUP + RUN)
         sums("second", GROUP, GROUP + RUN)
         quantise("first", both)
+        second_rows = first_layer_by_token(1, "second_rows", 0)
+        negated_rows = keep.tile([P, PACK, P], F32, name="negated_rows", tag="negated_rows", align_bytes=64)
+        nc.vector.tensor_scalar(negated_rows[:], second_rows[:], -1.0, None, ALU.mult)
         first_layer(0, GROUP + RUN, RUN, 4)
         gelu(0, GROUP + RUN, 2 * GROUP)
         gelu(1, GROUP + RUN, 2 * GROUP)
         sums("second", GROUP + RUN, 2 * GROUP)
-
-        first_acc = second_layer("first", 3)
-        second_rows = first_layer_by_token(1, "second_rows", 5)
-        first_rows = first_layer_by_token(0, "first_rows", 6)
-        last = stretches["last"][0]
-        first_layer(0, last, GROUP, 7)
-        first_layer(1, last, GROUP, 0)
-        negated_rows = keep.tile([P, PACK, P], F32, name="negated_rows", align_bytes=64)
-        nc.vector.tensor_scalar(negated_rows[:], second_rows[:], -1.0, None, ALU.mult)
+        first_rows = first_layer_by_token(0, "first_rows", 2)
+        first_layer(0, last, GROUP, 0)
+        first_layer(1, last, GROUP, 4)
+        first_acc = second_layer("first", 7)
         quantise("second", both)
-        low_acc = bank(1, [P, PACK, GROUP])
-        high_acc = bank(2, [P, PACK, GROUP])
+        low_acc = bank(5, [P, PACK, GROUP])
+        high_acc = bank(6, [P, PACK, GROUP])
         turn(low_acc, second_rows, True)
-        turn(low_acc, first_rows, False)
         turn(high_acc, negated_rows, True)
+        turn(low_acc, first_rows, False)
         turn(high_acc, first_rows, False)
-        second_acc = second_layer("second", 4)
-        store("first", first_acc, nc.sync)
+        second_acc = second_layer("second", 1)
         for lo in range(last, V, RUN):
             gelu(0, lo, lo + RUN)
             gelu(1, lo, lo + RUN)
@@ -244,10 +242,11 @@ def tile_picked_haar_gelu_p_kernel(
             nc.scalar.activation(bands["turned"][:, b], acc[:].rearrange("p t v -> p v t"), ACT.Copy)
         quantise("last", low)
         quantise("last", high)
-        last_acc = second_layer("last", 5)
+        last_acc = second_layer("last", 3)
         quantise("turned", low)
         quantise("turned", high)
+        store("first", first_acc, nc.sync)
         store("second", second_acc, nc.sync)
-        turned_acc = second_layer("turned", 6)
+        turned_acc = second_layer("turned", 2)
         store("last", last_acc, nc.sync)
         store("turned", turned_acc, nc.scalar)

@@ -51,6 +51,9 @@ def tile_picked_haar_gelu_p_kernel(
         table_scales = keep.tile([P, T], U8, name="table_scales", tag="scale_rows", align_bytes=64)
         nc.vector.memset(table_scales[:].bitcast(I32), 0)
         nc.sync.dma_start(out=table_scales[32:96:4, :].bitcast(I32), in_=x_scales[0].bitcast(I32))
+        band_w_rows = keep.tile([P, 2 * N], U8, name="band_w_rows", align_bytes=64)
+        nc.sync.dma_start(out=band_w_rows[32:96:4, :N].bitcast(I32), in_=w2_scales[0].bitcast(I32))
+        nc.sync.dma_start(out=band_w_rows[32:96:4, N:].bitcast(I32), in_=w3_scales[0].bitcast(I32))
         table_words = keep.tile([P, T], I32, name="table_words", align_bytes=64)
         nc.sync.dma_start(out=table_words[:], in_=words_of(x_words))
 
@@ -62,8 +65,7 @@ def tile_picked_haar_gelu_p_kernel(
 
         band_w_scales = keep.tile([P, 2 * N], U8, name="band_w_scales", tag="scale_rows", align_bytes=64)
         nc.vector.memset(band_w_scales[:].bitcast(I32), 0)
-        load_scale_rows([nc.sync], band_w_scales[:, 0:N], w2_scales[0])
-        load_scale_rows([nc.sync], band_w_scales[:, N : 2 * N], w3_scales[0])
+        load_scale_rows([nc.sync], band_w_scales, band_w_rows[32:96:4, :])
 
         identity = keep.tile([P, P], F32, name="identity", align_bytes=64)
         make_identity(nc, identity[:])
@@ -96,14 +98,14 @@ def tile_picked_haar_gelu_p_kernel(
         nc.sync.dma_start(out=band_w_words[:, 0, :], in_=words_of(w2_words))
         nc.sync.dma_start(out=band_w_words[:, 1, :], in_=words_of(w3_words))
 
-        early_words = keep.tile([P, V + GROUP], U32, name="early_words", align_bytes=64)
+        early_words = keep.tile([P, V + RUN], U32, name="early_words", align_bytes=64)
         late_words = keep.tile([P, V], U32, name="late_words", align_bytes=64)
-        for picked, first, count in ((early_words, 0, V + GROUP), (late_words, V, V)):
+        for picked, first, count in ((early_words, 0, V + RUN), (late_words, V, V)):
             entries = offsets[:, first // 16 : (first + count) // 16]
             nc.vector.tensor_copy(picked[:], table_words[:].bitcast(U32).indirect(entries))
 
         hidden = keep.tile([P, 2, V, PACK], F32, name="hidden")
-        stretches = {"first": (0, GROUP), "second": (GROUP, GROUP), "turned": (2 * GROUP, GROUP), "last": (3 * GROUP, GROUP)}
+        stretches = {"first": (0, GROUP), "second": (GROUP, GROUP), "third": (2 * GROUP, GROUP), "turned": (3 * GROUP, GROUP)}
         bands = {k: keep.tile([P, 2, n, PACK], BF16, name=f"bands_{k}", align_bytes=64) for k, (f, n) in stretches.items()}
         codes = {k: keep.tile([P, 2, n], U32, name=f"codes_{k}", align_bytes=64) for k, (f, n) in stretches.items()}
         scales = {k: keep.tile([P, 2, n], U8, name=f"scales_{k}", align_bytes=64) for k, (f, n) in stretches.items()}
@@ -111,7 +113,7 @@ def tile_picked_haar_gelu_p_kernel(
         banks = {}
 
         def picked_words(entry, count):
-            if entry < V + GROUP:
+            if entry < V + RUN:
                 return early_words[:, entry : entry + count].bitcast(FP8X4)
             return late_words[:, entry - V : entry - V + count].bitcast(FP8X4)
 
@@ -136,6 +138,24 @@ def tile_picked_haar_gelu_p_kernel(
             nc.scalar.activation(
                 hidden[:, d, lo:hi], acc[:].rearrange("p t v -> p v t")[:, lo - first : hi - first], ACT.Gelu_apprx_tanh
             )
+
+        def first_layer_of_pairs(first, number):
+            acc = bank(number, [P, 2, PACK, RUN])
+            for d in range(2):
+                entry = d * V + first
+                for t in range(PACK):
+                    nc.tensor.matmul_mx(
+                        out=acc[:, d, t],
+                        lhsT=w1_codes[:, t * P : (t + 1) * P].bitcast(FP8X4),
+                        lhsT_scale=w1_scales[:, t * P : (t + 1) * P],
+                        rhs=picked_words(entry, RUN),
+                        rhs_scale=picked_scales[:, entry : entry + RUN],
+                        start=True,
+                        stop=True,
+                    )
+            pairs = keep.tile([P, 2, RUN, PACK], F32, name="pairs")
+            nc.scalar.activation(pairs[:], acc[:].rearrange("p d t v -> p d v t"), ACT.Gelu_apprx_tanh)
+            return pairs
 
         def first_layer_by_token(d, name, number):
             acc = bank(number, [P, H])
@@ -198,55 +218,53 @@ def tile_picked_haar_gelu_p_kernel(
             queue.dma_start(out=out[:, first : first + count], in_=result[:])
 
         low, high, both = slice(0, 1), slice(1, 2), slice(0, 2)
-        last = stretches["last"][0]
         first_layer(0, 0, RUN, 0)
         gelu(0, 0, RUN)
-        first_layer(1, 0, GROUP, 1)
+        first_layer(1, 0, RUN, 1)
         gelu(1, 0, HEAD)
         sums("first", 0, HEAD)
         gelu(1, HEAD, RUN)
         sums("first", HEAD, RUN)
         first_layer(0, RUN, GROUP, 2)
-        gelu(0, RUN, GROUP)
-        gelu(1, RUN, GROUP)
-        sums("first", RUN, GROUP)
-        gelu(0, GROUP, GROUP + RUN)
-        first_layer(1, GROUP, GROUP, 3)
-        gelu(1, GROUP, GROUP + RUN)
-        sums("second", GROUP, GROUP + RUN)
-        quantise("first", both)
-        second_rows = first_layer_by_token(1, "second_rows", 0)
+        gelu(0, RUN, 3 * RUN)
+        first_layer(1, RUN, GROUP, 3)
+        gelu(1, RUN, 2 * RUN)
+        sums("first", RUN, 2 * RUN)
+        gelu(1, 2 * RUN, 3 * RUN)
+        sums("second", 2 * RUN, 3 * RUN)
+        second_rows = first_layer_by_token(1, "second_rows", 4)
         negated_rows = keep.tile([P, PACK, P], F32, name="negated_rows", tag="negated_rows", align_bytes=64)
         nc.vector.tensor_scalar(negated_rows[:], second_rows[:], -1.0, None, ALU.mult)
-        first_layer(0, GROUP + RUN, RUN, 4)
-        gelu(0, GROUP + RUN, 2 * GROUP)
-        gelu(1, GROUP + RUN, 2 * GROUP)
-        sums("second", GROUP + RUN, 2 * GROUP)
+        quantise("first", both)
+        pairs = first_layer_of_pairs(3 * RUN, 0)
+        for b, op in enumerate((ALU.add, ALU.subtract)):
+            nc.vector.tensor_tensor(bands["second"][:, b, RUN:], pairs[:, 0], pairs[:, 1], op)
         first_rows = first_layer_by_token(0, "first_rows", 2)
-        first_layer(0, last, GROUP, 0)
-        first_layer(1, last, GROUP, 4)
-        first_acc = second_layer("first", 7)
-        quantise("second", both)
+        first_layer(0, 4 * RUN, GROUP, 3)
+        first_layer(1, 4 * RUN, GROUP, 4)
+        quantise("second", low)
+        quantise("second", high)
         low_acc = bank(5, [P, PACK, GROUP])
         high_acc = bank(6, [P, PACK, GROUP])
         turn(low_acc, second_rows, True)
         turn(high_acc, negated_rows, True)
         turn(low_acc, first_rows, False)
         turn(high_acc, first_rows, False)
-        second_acc = second_layer("second", 1)
-        for lo in range(last, V, RUN):
+        for lo in (4 * RUN, 5 * RUN):
             gelu(0, lo, lo + RUN)
             gelu(1, lo, lo + RUN)
-            sums("last", lo, lo + RUN)
+            sums("third", lo, lo + RUN)
+        first_acc = second_layer("first", 3)
+        second_acc = second_layer("second", 4)
         for b, acc in enumerate((low_acc, high_acc)):
             nc.scalar.activation(bands["turned"][:, b], acc[:].rearrange("p t v -> p v t"), ACT.Copy)
-        quantise("last", low)
-        quantise("last", high)
-        last_acc = second_layer("last", 3)
+        quantise("third", low)
+        quantise("third", high)
+        third_acc = second_layer("third", 0)
         quantise("turned", low)
         quantise("turned", high)
         store("first", first_acc, nc.sync)
         store("second", second_acc, nc.sync)
         turned_acc = second_layer("turned", 2)
-        store("last", last_acc, nc.sync)
+        store("third", third_acc, nc.sync)
         store("turned", turned_acc, nc.scalar)

@@ -21,6 +21,7 @@ PACK = 4
 RUN = 64
 GROUP = 128
 HEAD = 32
+OPENING = 80
 WARM_WIDTHS = (512, 512, 256)
 
 
@@ -98,9 +99,9 @@ def tile_picked_haar_gelu_p_kernel(
         nc.sync.dma_start(out=band_w_words[:, 0, :], in_=words_of(w2_words))
         nc.sync.dma_start(out=band_w_words[:, 1, :], in_=words_of(w3_words))
 
-        early_words = keep.tile([P, V + RUN], U32, name="early_words", align_bytes=64)
+        early_words = keep.tile([P, V + GROUP], U32, name="early_words", align_bytes=64)
         late_words = keep.tile([P, V], U32, name="late_words", align_bytes=64)
-        for picked, first, count in ((early_words, 0, V + RUN), (late_words, V, V)):
+        for picked, first, count in ((early_words, 0, V + GROUP), (late_words, V, V)):
             entries = offsets[:, first // 16 : (first + count) // 16]
             nc.vector.tensor_copy(picked[:], table_words[:].bitcast(U32).indirect(entries))
 
@@ -113,7 +114,7 @@ def tile_picked_haar_gelu_p_kernel(
         banks = {}
 
         def picked_words(entry, count):
-            if entry < V + RUN:
+            if entry < V + GROUP:
                 return early_words[:, entry : entry + count].bitcast(FP8X4)
             return late_words[:, entry - V : entry - V + count].bitcast(FP8X4)
 
@@ -138,24 +139,6 @@ def tile_picked_haar_gelu_p_kernel(
             nc.scalar.activation(
                 hidden[:, d, lo:hi], acc[:].rearrange("p t v -> p v t")[:, lo - first : hi - first], ACT.Gelu_apprx_tanh
             )
-
-        def first_layer_of_pairs(first, number):
-            acc = bank(number, [P, 2, PACK, RUN])
-            for d in range(2):
-                entry = d * V + first
-                for t in range(PACK):
-                    nc.tensor.matmul_mx(
-                        out=acc[:, d, t],
-                        lhsT=w1_codes[:, t * P : (t + 1) * P].bitcast(FP8X4),
-                        lhsT_scale=w1_scales[:, t * P : (t + 1) * P],
-                        rhs=picked_words(entry, RUN),
-                        rhs_scale=picked_scales[:, entry : entry + RUN],
-                        start=True,
-                        stop=True,
-                    )
-            pairs = keep.tile([P, 2, RUN, PACK], F32, name="pairs")
-            nc.scalar.activation(pairs[:], acc[:].rearrange("p d t v -> p d v t"), ACT.Gelu_apprx_tanh)
-            return pairs
 
         def first_layer_by_token(d, name, number):
             acc = bank(number, [P, H])
@@ -218,34 +201,35 @@ def tile_picked_haar_gelu_p_kernel(
             queue.dma_start(out=out[:, first : first + count], in_=result[:])
 
         low, high, both = slice(0, 1), slice(1, 2), slice(0, 2)
-        first_layer(0, 0, RUN, 0)
-        gelu(0, 0, RUN)
-        first_layer(1, 0, RUN, 1)
+        first_layer(0, 0, GROUP, 0)
+        gelu(0, 0, OPENING)
+        first_layer(1, 0, GROUP, 1)
         gelu(1, 0, HEAD)
         sums("first", 0, HEAD)
-        gelu(1, HEAD, RUN)
-        sums("first", HEAD, RUN)
-        first_layer(0, RUN, GROUP, 2)
-        gelu(0, RUN, 3 * RUN)
-        first_layer(1, RUN, GROUP, 3)
-        gelu(1, RUN, 2 * RUN)
-        sums("first", RUN, 2 * RUN)
+        gelu(1, HEAD, OPENING)
+        sums("first", HEAD, OPENING)
+        gelu(0, OPENING, GROUP)
+        gelu(1, OPENING, GROUP)
+        sums("first", OPENING, GROUP)
+        first_layer(0, GROUP, GROUP, 2)
+        gelu(0, 2 * RUN, 3 * RUN)
+        first_layer(1, GROUP, GROUP, 3)
         gelu(1, 2 * RUN, 3 * RUN)
         sums("second", 2 * RUN, 3 * RUN)
+        quantise("first", both)
         second_rows = first_layer_by_token(1, "second_rows", 4)
         negated_rows = keep.tile([P, PACK, P], F32, name="negated_rows", tag="negated_rows", align_bytes=64)
         nc.vector.tensor_scalar(negated_rows[:], second_rows[:], -1.0, None, ALU.mult)
-        quantise("first", both)
-        pairs = first_layer_of_pairs(3 * RUN, 0)
-        for b, op in enumerate((ALU.add, ALU.subtract)):
-            nc.vector.tensor_tensor(bands["second"][:, b, RUN:], pairs[:, 0], pairs[:, 1], op)
-        first_rows = first_layer_by_token(0, "first_rows", 2)
-        first_layer(0, 4 * RUN, GROUP, 3)
-        first_layer(1, 4 * RUN, GROUP, 4)
+        gelu(0, 3 * RUN, 4 * RUN)
+        gelu(1, 3 * RUN, 4 * RUN)
+        sums("second", 3 * RUN, 4 * RUN)
+        first_rows = first_layer_by_token(0, "first_rows", 1)
+        first_layer(0, 2 * GROUP, GROUP, 4)
+        first_layer(1, 2 * GROUP, GROUP, 2)
         quantise("second", low)
         quantise("second", high)
-        low_acc = bank(5, [P, PACK, GROUP])
-        high_acc = bank(6, [P, PACK, GROUP])
+        low_acc = bank(3, [P, PACK, GROUP])
+        high_acc = bank(5, [P, PACK, GROUP])
         turn(low_acc, second_rows, True)
         turn(high_acc, negated_rows, True)
         turn(low_acc, first_rows, False)
@@ -254,8 +238,8 @@ def tile_picked_haar_gelu_p_kernel(
             gelu(0, lo, lo + RUN)
             gelu(1, lo, lo + RUN)
             sums("third", lo, lo + RUN)
-        first_acc = second_layer("first", 3)
-        second_acc = second_layer("second", 4)
+        first_acc = second_layer("first", 4)
+        second_acc = second_layer("second", 2)
         for b, acc in enumerate((low_acc, high_acc)):
             nc.scalar.activation(bands["turned"][:, b], acc[:].rearrange("p t v -> p v t"), ACT.Copy)
         quantise("third", low)
@@ -265,6 +249,6 @@ def tile_picked_haar_gelu_p_kernel(
         quantise("turned", high)
         store("first", first_acc, nc.sync)
         store("second", second_acc, nc.sync)
-        turned_acc = second_layer("turned", 2)
+        turned_acc = second_layer("turned", 1)
         store("third", third_acc, nc.sync)
         store("turned", turned_acc, nc.scalar)

@@ -22,6 +22,7 @@ RUN = 64
 GROUP = 128
 HEAD = 32
 OPENING = 80
+VECTOR_QUADS = 24
 WARM_WIDTHS = (512, 512, 256)
 
 
@@ -72,9 +73,10 @@ def tile_picked_haar_gelu_p_kernel(
         make_identity(nc, identity[:])
 
         w1_grouped = keep.tile([P, PACK, P, PACK], BF16, name="w1_grouped", align_bytes=64)
-        nc.scalar.copy(
-            w1_grouped[:].rearrange("p t m j -> p m t j"), w1_raw[:].rearrange("p j (m t) -> p m t j", t=PACK)
-        )
+        dealt = w1_grouped[:].rearrange("p t m j -> p m t j")
+        rows_by_quad = w1_raw[:].rearrange("p j (m t) -> p m t j", t=PACK)
+        nc.vector.tensor_copy(dealt[:, :VECTOR_QUADS], rows_by_quad[:, :VECTOR_QUADS])
+        nc.scalar.copy(dealt[:, VECTOR_QUADS:], rows_by_quad[:, VECTOR_QUADS:])
         w1_codes = keep.tile([P, PACK * P], U32, name="w1_codes", align_bytes=64)
         w1_scales = keep.tile([P, PACK * P], U8, name="w1_scales", align_bytes=64)
         nc.vector.quantize_mx(

@@ -22,7 +22,7 @@ RUN = 64
 GROUP = 128
 HEAD = 32
 OPENING = 80
-VECTOR_QUADS = 24
+VECTOR_QUADS = 64
 WARM_WIDTHS = (512, 512, 256)
 
 

@@ -21,8 +21,7 @@ PACK = 4
 RUN = 64
 GROUP = 128
 HEAD = 32
-OPENING = 80
-VECTOR_QUADS = 64
+VECTOR_QUADS = 96
 WARM_WIDTHS = (512, 512, 256)
 
 
@@ -101,7 +100,7 @@ def tile_picked_haar_gelu_p_kernel(
         nc.sync.dma_start(out=band_w_words[:, 0, :], in_=words_of(w2_words))
         nc.sync.dma_start(out=band_w_words[:, 1, :], in_=words_of(w3_words))
 
-        early_words = keep.tile([P, V + GROUP], U32, name="early_words", align_bytes=64)
+        early_words = keep.tile([P, V + GROUP], U32, name="early_words", tag="early_words", align_bytes=64)
         late_words = keep.tile([P, V], U32, name="late_words", align_bytes=64)
         for picked, first, count in ((early_words, 0, V + GROUP), (late_words, V, V)):
             entries = offsets[:, first // 16 : (first + count) // 16]
@@ -110,7 +109,7 @@ def tile_picked_haar_gelu_p_kernel(
         hidden = keep.tile([P, 2, V, PACK], F32, name="hidden")
         stretches = {"first": (0, GROUP), "second": (GROUP, GROUP), "third": (2 * GROUP, GROUP), "turned": (3 * GROUP, GROUP)}
         bands = {k: keep.tile([P, 2, n, PACK], BF16, name=f"bands_{k}", align_bytes=64) for k, (f, n) in stretches.items()}
-        codes = {k: keep.tile([P, 2, n], U32, name=f"codes_{k}", align_bytes=64) for k, (f, n) in stretches.items()}
+        codes = {}
         scales = {k: keep.tile([P, 2, n], U8, name=f"scales_{k}", align_bytes=64) for k, (f, n) in stretches.items()}
 
         banks = {}
@@ -142,21 +141,20 @@ def tile_picked_haar_gelu_p_kernel(
                 hidden[:, d, lo:hi], acc[:].rearrange("p t v -> p v t")[:, lo - first : hi - first], ACT.Gelu_apprx_tanh
             )
 
-        def first_layer_by_token(d, name, number):
-            acc = bank(number, [P, H])
+        def first_layer_by_token(d, rows, tiles, number):
+            columns = slice(tiles.start * P, tiles.stop * P)
+            acc = bank(number, [P, columns.stop - columns.start])
             entry = d * V + stretches["turned"][0]
             nc.tensor.matmul_mx(
                 out=acc[:],
                 lhsT=picked_words(entry, GROUP),
                 lhsT_scale=picked_scales[:, entry : entry + GROUP],
-                rhs=w1_codes[:].bitcast(FP8X4),
-                rhs_scale=w1_scales[:],
+                rhs=w1_codes[:, columns].bitcast(FP8X4),
+                rhs_scale=w1_scales[:, columns],
                 start=True,
                 stop=True,
             )
-            rows = keep.tile([P, PACK, P], F32, name=name, tag=name, align_bytes=64)
-            nc.scalar.activation(rows[:].rearrange("v t m -> v (t m)"), acc[:], ACT.Gelu_apprx_tanh)
-            return rows
+            nc.scalar.activation(rows[:, tiles].rearrange("v t m -> v (t m)"), acc[:], ACT.Gelu_apprx_tanh)
 
         def turn(acc, rows, opens):
             for t in range(PACK):
@@ -175,82 +173,82 @@ def tile_picked_haar_gelu_p_kernel(
                 nc.vector.tensor_tensor(bands[k][:, b, lo - first : hi - first], hidden[:, 0, lo:hi], hidden[:, 1, lo:hi], op)
 
         def quantise(k, b):
+            if k not in codes:
+                tag = "early_words" if k == "first" else f"codes_{k}"
+                codes[k] = keep.tile([P, 2, GROUP], U32, name=f"codes_{k}", tag=tag, align_bytes=64)
             nc.vector.quantize_mx(
                 out=codes[k][:, b].rearrange("p b v -> p (b v)").bitcast(FP8X4),
                 scales=scales[k][:, b].rearrange("p b v -> p (b v)"),
                 in_=bands[k][:, b].rearrange("p b v t -> p (b v t)"),
             )
 
-        def second_layer(k, number):
-            acc = bank(number, [N, GROUP])
-            for b in range(2):
-                nc.tensor.matmul_mx(
-                    out=acc[:],
-                    lhsT=band_w_words[:, b, :].bitcast(FP8X4),
-                    lhsT_scale=band_w_scales[:, b * N : (b + 1) * N],
-                    rhs=codes[k][:, b].bitcast(FP8X4),
-                    rhs_scale=scales[k][:, b],
-                    start=(b == 0),
-                    stop=(b == 1),
-                )
-            return acc
+        def second_pass(k, acc, b):
+            nc.tensor.matmul_mx(
+                out=acc[:],
+                lhsT=band_w_words[:, b, :].bitcast(FP8X4),
+                lhsT_scale=band_w_scales[:, b * N : (b + 1) * N],
+                rhs=codes[k][:, b].bitcast(FP8X4),
+                rhs_scale=scales[k][:, b],
+                start=(b == 0),
+                stop=(b == 1),
+            )
 
         def store(k, acc, queue):
             first, count = stretches[k]
-            tag = {"first": "first_rows", "second": "negated_rows"}.get(k, f"result_{k}")
+            tag = {"first": "second_rows", "second": "first_rows"}.get(k, f"result_{k}")
             result = keep.tile([N, count], F32, name=f"result_{k}", tag=tag, align_bytes=64)
             nc.scalar.activation(result[:], acc[:], ACT.Copy, scale=0.5)
             queue.dma_start(out=out[:, first : first + count], in_=result[:])
 
         low, high, both = slice(0, 1), slice(1, 2), slice(0, 2)
-        first_layer(0, 0, GROUP, 0)
-        gelu(0, 0, OPENING)
-        first_layer(1, 0, GROUP, 1)
+        first_rows = keep.tile([P, PACK, P], F32, name="first_rows", tag="first_rows", align_bytes=64)
+        first_layer_by_token(0, first_rows, slice(0, 2), 0)
+        first_layer_by_token(0, first_rows, slice(2, 4), 1)
+        negated_rows = keep.tile([P, PACK, P], F32, name="negated_rows", align_bytes=64)
+        nc.vector.tensor_scalar(negated_rows[:], first_rows[:], -1.0, None, ALU.mult)
+        first_layer(0, 0, GROUP, 2)
+        gelu(0, 0, RUN)
+        first_layer(1, 0, GROUP, 3)
         gelu(1, 0, HEAD)
         sums("first", 0, HEAD)
-        gelu(1, HEAD, OPENING)
-        sums("first", HEAD, OPENING)
-        gelu(0, OPENING, GROUP)
-        gelu(1, OPENING, GROUP)
-        sums("first", OPENING, GROUP)
-        first_layer(0, GROUP, GROUP, 2)
-        gelu(0, 2 * RUN, 3 * RUN)
-        first_layer(1, GROUP, GROUP, 3)
-        gelu(1, 2 * RUN, 3 * RUN)
-        sums("second", 2 * RUN, 3 * RUN)
-        quantise("first", both)
-        second_rows = first_layer_by_token(1, "second_rows", 4)
-        negated_rows = keep.tile([P, PACK, P], F32, name="negated_rows", tag="negated_rows", align_bytes=64)
-        nc.vector.tensor_scalar(negated_rows[:], second_rows[:], -1.0, None, ALU.mult)
-        gelu(0, 3 * RUN, 4 * RUN)
-        gelu(1, 3 * RUN, 4 * RUN)
-        sums("second", 3 * RUN, 4 * RUN)
-        first_rows = first_layer_by_token(0, "first_rows", 1)
-        first_layer(0, 2 * GROUP, GROUP, 4)
-        first_layer(1, 2 * GROUP, GROUP, 2)
-        quantise("second", low)
-        quantise("second", high)
-        low_acc = bank(3, [P, PACK, GROUP])
-        high_acc = bank(5, [P, PACK, GROUP])
-        turn(low_acc, second_rows, True)
+        gelu(1, HEAD, RUN)
+        sums("first", HEAD, RUN)
+        gelu(0, RUN, GROUP)
+        gelu(1, RUN, GROUP)
+        sums("first", RUN, GROUP)
+        first_layer(0, GROUP, GROUP, 4)
+        first_layer(1, GROUP, GROUP, 5)
+        low_acc = bank(6, [P, PACK, GROUP])
+        high_acc = bank(7, [P, PACK, GROUP])
+        turn(low_acc, first_rows, True)
         turn(high_acc, negated_rows, True)
-        turn(low_acc, first_rows, False)
-        turn(high_acc, first_rows, False)
+        for lo in (2 * RUN, 3 * RUN):
+            gelu(0, lo, lo + RUN)
+            gelu(1, lo, lo + RUN)
+            sums("second", lo, lo + RUN)
+        second_rows = keep.tile([P, PACK, P], F32, name="second_rows", tag="second_rows", align_bytes=64)
+        first_layer_by_token(1, second_rows, slice(0, 4), 3)
+        first_layer(0, 2 * GROUP, GROUP, 4)
+        first_layer(1, 2 * GROUP, GROUP, 5)
+        quantise("first", both)
+        quantise("second", both)
+        turn(low_acc, second_rows, False)
+        turn(high_acc, second_rows, False)
         for lo in (4 * RUN, 5 * RUN):
             gelu(0, lo, lo + RUN)
             gelu(1, lo, lo + RUN)
             sums("third", lo, lo + RUN)
-        first_acc = second_layer("first", 4)
-        second_acc = second_layer("second", 2)
-        for b, acc in enumerate((low_acc, high_acc)):
-            nc.scalar.activation(bands["turned"][:, b], acc[:].rearrange("p t v -> p v t"), ACT.Copy)
-        quantise("third", low)
-        quantise("third", high)
-        third_acc = second_layer("third", 0)
-        quantise("turned", low)
-        quantise("turned", high)
-        store("first", first_acc, nc.sync)
-        store("second", second_acc, nc.sync)
-        turned_acc = second_layer("turned", 1)
-        store("third", third_acc, nc.sync)
-        store("turned", turned_acc, nc.scalar)
+        accs = {k: bank(number, [N, GROUP]) for k, number in (("first", 4), ("second", 5), ("third", 0), ("turned", 1))}
+        for k in ("first", "second"):
+            second_pass(k, accs[k], 0)
+            second_pass(k, accs[k], 1)
+        for b, acc, sign in ((0, low_acc, 1.0), (1, high_acc, -1.0)):
+            nc.scalar.activation(bands["turned"][:, b], acc[:].rearrange("p t v -> p v t"), ACT.Copy, scale=sign)
+        for b, band in enumerate((low, high)):
+            for k in ("third", "turned"):
+                quantise(k, band)
+                second_pass(k, accs[k], b)
+        store("first", accs["first"], nc.sync)
+        store("second", accs["second"], nc.sync)
+        store("third", accs["third"], nc.sync)
+        store("turned", accs["turned"], nc.scalar)

@@ -20,7 +20,6 @@ P = 128
 PACK = 4
 RUN = 64
 GROUP = 128
-HEAD = 32
 VECTOR_QUADS = 96
 WARM_WIDTHS = (512, 512, 256)
 
@@ -100,9 +99,9 @@ def tile_picked_haar_gelu_p_kernel(
         nc.sync.dma_start(out=band_w_words[:, 0, :], in_=words_of(w2_words))
         nc.sync.dma_start(out=band_w_words[:, 1, :], in_=words_of(w3_words))
 
-        early_words = keep.tile([P, V + GROUP], U32, name="early_words", tag="early_words", align_bytes=64)
+        early_words = keep.tile([P, V + RUN], U32, name="early_words", tag="early_words", align_bytes=64)
         late_words = keep.tile([P, V], U32, name="late_words", align_bytes=64)
-        for picked, first, count in ((early_words, 0, V + GROUP), (late_words, V, V)):
+        for picked, first, count in ((early_words, 0, V + RUN), (late_words, V, V)):
             entries = offsets[:, first // 16 : (first + count) // 16]
             nc.vector.tensor_copy(picked[:], table_words[:].bitcast(U32).indirect(entries))
 
@@ -115,7 +114,7 @@ def tile_picked_haar_gelu_p_kernel(
         banks = {}
 
         def picked_words(entry, count):
-            if entry < V + GROUP:
+            if entry < V + RUN:
                 return early_words[:, entry : entry + count].bitcast(FP8X4)
             return late_words[:, entry - V : entry - V + count].bitcast(FP8X4)
 
@@ -208,16 +207,15 @@ def tile_picked_haar_gelu_p_kernel(
         nc.vector.tensor_scalar(negated_rows[:], first_rows[:], -1.0, None, ALU.mult)
         first_layer(0, 0, GROUP, 2)
         gelu(0, 0, RUN)
-        first_layer(1, 0, GROUP, 3)
-        gelu(1, 0, HEAD)
-        sums("first", 0, HEAD)
-        gelu(1, HEAD, RUN)
-        sums("first", HEAD, RUN)
-        gelu(0, RUN, GROUP)
-        gelu(1, RUN, GROUP)
-        sums("first", RUN, GROUP)
+        first_layer(1, 0, RUN, 3)
+        gelu(1, 0, RUN)
+        sums("first", 0, RUN)
+        gelu(0, RUN, 2 * RUN)
         first_layer(0, GROUP, GROUP, 4)
-        first_layer(1, GROUP, GROUP, 5)
+        first_layer(1, RUN, GROUP, 5)
+        gelu(1, RUN, 2 * RUN)
+        sums("first", RUN, 2 * RUN)
+        first_layer(1, 3 * RUN, GROUP, 0)
         low_acc = bank(6, [P, PACK, GROUP])
         high_acc = bank(7, [P, PACK, GROUP])
         turn(low_acc, first_rows, True)
@@ -229,7 +227,7 @@ def tile_picked_haar_gelu_p_kernel(
         second_rows = keep.tile([P, PACK, P], F32, name="second_rows", tag="second_rows", align_bytes=64)
         first_layer_by_token(1, second_rows, slice(0, 4), 3)
         first_layer(0, 2 * GROUP, GROUP, 4)
-        first_layer(1, 2 * GROUP, GROUP, 5)
+        first_layer(1, 5 * RUN, RUN, 5)
         quantise("first", both)
         quantise("second", both)
         turn(low_acc, second_rows, False)
@@ -238,7 +236,7 @@ def tile_picked_haar_gelu_p_kernel(
             gelu(0, lo, lo + RUN)
             gelu(1, lo, lo + RUN)
             sums("third", lo, lo + RUN)
-        accs = {k: bank(number, [N, GROUP]) for k, number in (("first", 4), ("second", 5), ("third", 0), ("turned", 1))}
+        accs = {k: bank(number, [N, GROUP]) for k, number in (("first", 4), ("second", 5), ("third", 2), ("turned", 1))}
         for k in ("first", "second"):
             second_pass(k, accs[k], 0)
             second_pass(k, accs[k], 1)

@@ -20,7 +20,7 @@ P = 128
 PACK = 4
 RUN = 64
 GROUP = 128
-VECTOR_QUADS = 96
+VECTOR_QUADS = 104
 WARM_WIDTHS = (512, 512, 256)
 
 

@@ -18,15 +18,15 @@ ALU = mybir.AluOpType
 
 P = 128
 PACK = 4
-RUN = 64
 GROUP = 128
-VECTOR_QUADS = 104
+QUARTER = 256
+VECTOR_QUADS = 24
 WARM_WIDTHS = (512, 512, 256)
 
 
-def load_scale_rows(queues, plane, rows):
+def load_scale_rows(queue, plane, rows):
     for r in range(4):
-        queues[r % len(queues)].dma_start(out=plane[r:P:32, :].bitcast(I32), in_=rows[r:16:4, :].bitcast(I32))
+        queue.dma_start(out=plane[r:P:32, :].bitcast(I32), in_=rows[r:16:4, :].bitcast(I32))
 
 
 def words_of(packed):
@@ -39,21 +39,19 @@ def tile_picked_haar_gelu_p_kernel(
     nc = tc.nc
     with ExitStack() as ctx:
         keep = ctx.enter_context(tc.tile_pool(name="keep", bufs=1))
+        reused = ctx.enter_context(tc.tile_pool(name="reused", bufs=1))
         psum = ctx.enter_context(tc.psum_pool(name="psum", bufs=1))
 
         def bank(number, shape):
             return psum.tile(shape, F32, name=f"bank{number}", tag=f"bank{number}")
 
-        w1_raw = keep.tile([P, PACK, H], F32, name="w1_raw", tag="staged", align_bytes=64)
+        w1_raw = keep.tile([P, PACK, H], F32, name="w1_raw", align_bytes=64)
         nc.sync.dma_start(out=w1_raw[:], in_=w1.rearrange("(p j) c -> p j c", j=PACK))
         offsets = keep.tile([P, S // 16], U16, name="offsets")
         nc.sync.dma_start(offsets[:], offs)
-        table_scales = keep.tile([P, T], U8, name="table_scales", tag="scale_rows", align_bytes=64)
+        table_scales = reused.tile([P, T], U8, name="table_scales", offset=0, align_bytes=64)
         nc.vector.memset(table_scales[:].bitcast(I32), 0)
         nc.sync.dma_start(out=table_scales[32:96:4, :].bitcast(I32), in_=x_scales[0].bitcast(I32))
-        band_w_rows = keep.tile([P, 2 * N], U8, name="band_w_rows", align_bytes=64)
-        nc.sync.dma_start(out=band_w_rows[32:96:4, :N].bitcast(I32), in_=w2_scales[0].bitcast(I32))
-        nc.sync.dma_start(out=band_w_rows[32:96:4, N:].bitcast(I32), in_=w3_scales[0].bitcast(I32))
         table_words = keep.tile([P, T], I32, name="table_words", align_bytes=64)
         nc.sync.dma_start(out=table_words[:], in_=words_of(x_words))
 
@@ -61,11 +59,7 @@ def tile_picked_haar_gelu_p_kernel(
         nc.vector.memset(picked_scales[:].bitcast(I32), 0)
         picked_rows = keep.tile([P, S], U8, name="picked_rows", align_bytes=64)
         nc.vector.tensor_copy(picked_rows[:], table_scales[:].indirect(offsets[:]))
-        load_scale_rows([nc.sync, nc.scalar], picked_scales, picked_rows[32:96:4, :])
-
-        band_w_scales = keep.tile([P, 2 * N], U8, name="band_w_scales", tag="scale_rows", align_bytes=64)
-        nc.vector.memset(band_w_scales[:].bitcast(I32), 0)
-        load_scale_rows([nc.sync], band_w_scales, band_w_rows[32:96:4, :])
+        load_scale_rows(nc.sync, picked_scales, picked_rows[32:96:4, :])
 
         identity = keep.tile([P, P], F32, name="identity", align_bytes=64)
         make_identity(nc, identity[:])
@@ -95,59 +89,56 @@ def tile_picked_haar_gelu_p_kernel(
                 stop=True,
             )
 
-        band_w_words = keep.tile([P, 2, N], I32, name="band_w_words", tag="staged", align_bytes=64)
+        band_w_words = reused.tile([P, 2, N], I32, name="band_w_words", offset=0, align_bytes=64)
         nc.sync.dma_start(out=band_w_words[:, 0, :], in_=words_of(w2_words))
         nc.sync.dma_start(out=band_w_words[:, 1, :], in_=words_of(w3_words))
+        band_w_scales = reused.tile([P, 2 * N], U8, name="band_w_scales", offset=2 * N * 4, align_bytes=64)
+        nc.gpsimd.memset(band_w_scales[:].bitcast(I32), 0)
+        load_scale_rows(nc.sync, band_w_scales[:, :N], w2_scales[0])
+        load_scale_rows(nc.sync, band_w_scales[:, N:], w3_scales[0])
 
-        early_words = keep.tile([P, V + RUN], U32, name="early_words", tag="early_words", align_bytes=64)
-        late_words = keep.tile([P, V], U32, name="late_words", align_bytes=64)
-        for picked, first, count in ((early_words, 0, V + RUN), (late_words, V, V)):
-            entries = offsets[:, first // 16 : (first + count) // 16]
-            nc.vector.tensor_copy(picked[:], table_words[:].bitcast(U32).indirect(entries))
+        picked_words = {}
+        for half in range(2):
+            for d in range(2):
+                first = d * V + half * QUARTER
+                picked_words[d, half] = keep.tile([P, QUARTER], U32, name=f"picked_words_{d}{half}", align_bytes=64)
+                entries = offsets[:, first // 16 : (first + QUARTER) // 16]
+                nc.vector.tensor_copy(picked_words[d, half][:], table_words[:].bitcast(U32).indirect(entries))
 
-        hidden = keep.tile([P, 2, V, PACK], F32, name="hidden")
-        stretches = {"first": (0, GROUP), "second": (GROUP, GROUP), "third": (2 * GROUP, GROUP), "turned": (3 * GROUP, GROUP)}
-        bands = {k: keep.tile([P, 2, n, PACK], BF16, name=f"bands_{k}", align_bytes=64) for k, (f, n) in stretches.items()}
-        codes = {}
-        scales = {k: keep.tile([P, 2, n], U8, name=f"scales_{k}", align_bytes=64) for k, (f, n) in stretches.items()}
+        first_pair = {"turned": 0, "early": GROUP, "middle": 2 * GROUP, "late": 3 * GROUP}
+        hidden = {k: keep.tile([P, 2, GROUP, PACK], F32, name=f"hidden_{k}") for k in ("early", "middle", "late")}
+        bands = {k: keep.tile([P, 2, GROUP, PACK], BF16, name=f"bands_{k}", align_bytes=64) for k in first_pair}
+        codes = {k: keep.tile([P, 2, GROUP], U32, name=f"codes_{k}", align_bytes=64) for k in first_pair}
+        scales = {k: keep.tile([P, 2, GROUP], U8, name=f"scales_{k}", align_bytes=64) for k in first_pair}
 
-        banks = {}
+        def patches(d, k):
+            half, place = divmod(first_pair[k], QUARTER)
+            entry = d * V + first_pair[k]
+            return picked_words[d, half][:, place : place + GROUP].bitcast(FP8X4), picked_scales[:, entry : entry + GROUP]
 
-        def picked_words(entry, count):
-            if entry < V + RUN:
-                return early_words[:, entry : entry + count].bitcast(FP8X4)
-            return late_words[:, entry - V : entry - V + count].bitcast(FP8X4)
-
-        def first_layer(d, first, count, number):
-            acc = bank(number, [P, PACK, count])
-            entry = d * V + first
+        def layer_by_channel(d, k, number):
+            acc = bank(number, [P, PACK, GROUP])
+            words, plane = patches(d, k)
             for t in range(PACK):
                 nc.tensor.matmul_mx(
                     out=acc[:, t],
                     lhsT=w1_codes[:, t * P : (t + 1) * P].bitcast(FP8X4),
                     lhsT_scale=w1_scales[:, t * P : (t + 1) * P],
-                    rhs=picked_words(entry, count),
-                    rhs_scale=picked_scales[:, entry : entry + count],
+                    rhs=words,
+                    rhs_scale=plane,
                     start=True,
                     stop=True,
                 )
-            for v in range(first, first + count):
-                banks[d, v] = (acc, first)
+            nc.scalar.activation(hidden[k][:, d], acc[:].rearrange("p t v -> p v t"), ACT.Gelu_apprx_tanh)
 
-        def gelu(d, lo, hi):
-            acc, first = banks[d, lo]
-            nc.scalar.activation(
-                hidden[:, d, lo:hi], acc[:].rearrange("p t v -> p v t")[:, lo - first : hi - first], ACT.Gelu_apprx_tanh
-            )
-
-        def first_layer_by_token(d, rows, tiles, number):
+        def layer_by_patch(d, rows, tiles, number):
             columns = slice(tiles.start * P, tiles.stop * P)
             acc = bank(number, [P, columns.stop - columns.start])
-            entry = d * V + stretches["turned"][0]
+            words, plane = patches(d, "turned")
             nc.tensor.matmul_mx(
                 out=acc[:],
-                lhsT=picked_words(entry, GROUP),
-                lhsT_scale=picked_scales[:, entry : entry + GROUP],
+                lhsT=words,
+                lhsT_scale=plane,
                 rhs=w1_codes[:, columns].bitcast(FP8X4),
                 rhs_scale=w1_scales[:, columns],
                 start=True,
@@ -166,15 +157,11 @@ def tile_picked_haar_gelu_p_kernel(
                     stop=(not opens and t == PACK - 1),
                 )
 
-        def sums(k, lo, hi):
-            first = stretches[k][0]
+        def sums(k):
             for b, op in enumerate((ALU.add, ALU.subtract)):
-                nc.vector.tensor_tensor(bands[k][:, b, lo - first : hi - first], hidden[:, 0, lo:hi], hidden[:, 1, lo:hi], op)
+                nc.vector.tensor_tensor(bands[k][:, b], hidden[k][:, 0], hidden[k][:, 1], op)
 
         def quantise(k, b):
-            if k not in codes:
-                tag = "early_words" if k == "first" else f"codes_{k}"
-                codes[k] = keep.tile([P, 2, GROUP], U32, name=f"codes_{k}", tag=tag, align_bytes=64)
             nc.vector.quantize_mx(
                 out=codes[k][:, b].rearrange("p b v -> p (b v)").bitcast(FP8X4),
                 scales=scales[k][:, b].rearrange("p b v -> p (b v)"),
@@ -192,61 +179,47 @@ def tile_picked_haar_gelu_p_kernel(
                 stop=(b == 1),
             )
 
-        def store(k, acc, queue):
-            first, count = stretches[k]
-            tag = {"first": "second_rows", "second": "first_rows"}.get(k, f"result_{k}")
-            result = keep.tile([N, count], F32, name=f"result_{k}", tag=tag, align_bytes=64)
+        def store(k, acc, queue, tag):
+            result = keep.tile([N, GROUP], F32, name=f"result_{k}", tag=tag, align_bytes=64)
             nc.scalar.activation(result[:], acc[:], ACT.Copy, scale=0.5)
-            queue.dma_start(out=out[:, first : first + count], in_=result[:])
+            queue.dma_start(out=out[:, first_pair[k] : first_pair[k] + GROUP], in_=result[:])
 
         low, high, both = slice(0, 1), slice(1, 2), slice(0, 2)
         first_rows = keep.tile([P, PACK, P], F32, name="first_rows", tag="first_rows", align_bytes=64)
-        first_layer_by_token(0, first_rows, slice(0, 2), 0)
-        first_layer_by_token(0, first_rows, slice(2, 4), 1)
-        negated_rows = keep.tile([P, PACK, P], F32, name="negated_rows", align_bytes=64)
+        layer_by_patch(0, first_rows, slice(0, 2), 0)
+        layer_by_patch(0, first_rows, slice(2, 4), 1)
+        negated_rows = keep.tile([P, PACK, P], F32, name="negated_rows", tag="negated_rows", align_bytes=64)
+        layer_by_channel(0, "early", 2)
+        layer_by_channel(1, "early", 3)
         nc.vector.tensor_scalar(negated_rows[:], first_rows[:], -1.0, None, ALU.mult)
-        first_layer(0, 0, GROUP, 2)
-        gelu(0, 0, RUN)
-        first_layer(1, 0, RUN, 3)
-        gelu(1, 0, RUN)
-        sums("first", 0, RUN)
-        gelu(0, RUN, 2 * RUN)
-        first_layer(0, GROUP, GROUP, 4)
-        first_layer(1, RUN, GROUP, 5)
-        gelu(1, RUN, 2 * RUN)
-        sums("first", RUN, 2 * RUN)
-        first_layer(1, 3 * RUN, GROUP, 0)
+        sums("early")
+        layer_by_channel(0, "middle", 4)
+        layer_by_channel(1, "middle", 5)
         low_acc = bank(6, [P, PACK, GROUP])
         high_acc = bank(7, [P, PACK, GROUP])
         turn(low_acc, first_rows, True)
         turn(high_acc, negated_rows, True)
-        for lo in (2 * RUN, 3 * RUN):
-            gelu(0, lo, lo + RUN)
-            gelu(1, lo, lo + RUN)
-            sums("second", lo, lo + RUN)
+        sums("middle")
         second_rows = keep.tile([P, PACK, P], F32, name="second_rows", tag="second_rows", align_bytes=64)
-        first_layer_by_token(1, second_rows, slice(0, 4), 3)
-        first_layer(0, 2 * GROUP, GROUP, 4)
-        first_layer(1, 5 * RUN, RUN, 5)
-        quantise("first", both)
-        quantise("second", both)
+        layer_by_patch(1, second_rows, slice(0, 4), 2)
+        layer_by_channel(0, "late", 3)
+        layer_by_channel(1, "late", 4)
+        quantise("early", both)
+        quantise("middle", both)
         turn(low_acc, second_rows, False)
         turn(high_acc, second_rows, False)
-        for lo in (4 * RUN, 5 * RUN):
-            gelu(0, lo, lo + RUN)
-            gelu(1, lo, lo + RUN)
-            sums("third", lo, lo + RUN)
-        accs = {k: bank(number, [N, GROUP]) for k, number in (("first", 4), ("second", 5), ("third", 2), ("turned", 1))}
-        for k in ("first", "second"):
+        sums("late")
+        accs = {k: bank(number, [N, GROUP]) for k, number in (("early", 3), ("middle", 4), ("late", 0), ("turned", 1))}
+        for k in ("early", "middle"):
             second_pass(k, accs[k], 0)
             second_pass(k, accs[k], 1)
         for b, acc, sign in ((0, low_acc, 1.0), (1, high_acc, -1.0)):
             nc.scalar.activation(bands["turned"][:, b], acc[:].rearrange("p t v -> p v t"), ACT.Copy, scale=sign)
         for b, band in enumerate((low, high)):
-            for k in ("third", "turned"):
+            for k in ("turned", "late"):
                 quantise(k, band)
                 second_pass(k, accs[k], b)
-        store("first", accs["first"], nc.sync)
-        store("second", accs["second"], nc.sync)
-        store("third", accs["third"], nc.sync)
-        store("turned", accs["turned"], nc.scalar)
+        store("early", accs["early"], nc.sync, "second_rows")
+        store("middle", accs["middle"], nc.sync, "first_rows")
+        store("turned", accs["turned"], nc.sync, "result_turned")
+        store("late", accs["late"], nc.scalar, "result_late")

@@ -94,8 +94,8 @@ def tile_picked_haar_gelu_p_kernel(
         nc.sync.dma_start(out=band_w_words[:, 1, :], in_=words_of(w3_words))
         band_w_scales = reused.tile([P, 2 * N], U8, name="band_w_scales", offset=2 * N * 4, align_bytes=64)
         nc.gpsimd.memset(band_w_scales[:].bitcast(I32), 0)
-        load_scale_rows(nc.sync, band_w_scales[:, :N], w2_scales[0])
         load_scale_rows(nc.sync, band_w_scales[:, N:], w3_scales[0])
+        load_scale_rows(nc.sync, band_w_scales[:, :N], w2_scales[0])
 
         picked_words = {}
         for half in range(2):
@@ -129,9 +129,12 @@ def tile_picked_haar_gelu_p_kernel(
                     start=True,
                     stop=True,
                 )
+            return acc
+
+        def gelu_by_channel(d, k, acc):
             nc.scalar.activation(hidden[k][:, d], acc[:].rearrange("p t v -> p v t"), ACT.Gelu_apprx_tanh)
 
-        def layer_by_patch(d, rows, tiles, number):
+        def layer_by_patch(d, tiles, number):
             columns = slice(tiles.start * P, tiles.stop * P)
             acc = bank(number, [P, columns.stop - columns.start])
             words, plane = patches(d, "turned")
@@ -144,6 +147,9 @@ def tile_picked_haar_gelu_p_kernel(
                 start=True,
                 stop=True,
             )
+            return acc
+
+        def gelu_by_patch(rows, tiles, acc):
             nc.scalar.activation(rows[:, tiles].rearrange("v t m -> v (t m)"), acc[:], ACT.Gelu_apprx_tanh)
 
         def turn(acc, rows, opens):
@@ -186,30 +192,31 @@ def tile_picked_haar_gelu_p_kernel(
 
         low, high, both = slice(0, 1), slice(1, 2), slice(0, 2)
         first_rows = keep.tile([P, PACK, P], F32, name="first_rows", tag="first_rows", align_bytes=64)
-        layer_by_patch(0, first_rows, slice(0, 2), 0)
-        layer_by_patch(0, first_rows, slice(2, 4), 1)
+        for number, tiles in enumerate((slice(0, 2), slice(2, 4))):
+            gelu_by_patch(first_rows, tiles, layer_by_patch(0, tiles, number))
         negated_rows = keep.tile([P, PACK, P], F32, name="negated_rows", tag="negated_rows", align_bytes=64)
-        layer_by_channel(0, "early", 2)
-        layer_by_channel(1, "early", 3)
+        for d in range(2):
+            gelu_by_channel(d, "early", layer_by_channel(d, "early", 2 + d))
         nc.vector.tensor_scalar(negated_rows[:], first_rows[:], -1.0, None, ALU.mult)
         sums("early")
-        layer_by_channel(0, "middle", 4)
-        layer_by_channel(1, "middle", 5)
+        gelu_by_channel(0, "middle", layer_by_channel(0, "middle", 4))
         low_acc = bank(6, [P, PACK, GROUP])
-        high_acc = bank(7, [P, PACK, GROUP])
         turn(low_acc, first_rows, True)
-        turn(high_acc, negated_rows, True)
+        gelu_by_channel(1, "middle", layer_by_channel(1, "middle", 1))
         sums("middle")
         second_rows = keep.tile([P, PACK, P], F32, name="second_rows", tag="second_rows", align_bytes=64)
-        layer_by_patch(1, second_rows, slice(0, 4), 2)
-        layer_by_channel(0, "late", 3)
-        layer_by_channel(1, "late", 4)
+        gelu_by_patch(second_rows, slice(0, 4), layer_by_patch(1, slice(0, 4), 2))
+        high_acc = bank(7, [P, PACK, GROUP])
+        turn(high_acc, negated_rows, True)
+        late_accs = [layer_by_channel(d, "late", 3 + d) for d in range(2)]
         quantise("early", both)
         quantise("middle", both)
         turn(low_acc, second_rows, False)
         turn(high_acc, second_rows, False)
+        for d in range(2):
+            gelu_by_channel(d, "late", late_accs[d])
         sums("late")
-        accs = {k: bank(number, [N, GROUP]) for k, number in (("early", 3), ("middle", 4), ("late", 0), ("turned", 1))}
+        accs = {k: bank(number, [N, GROUP]) for k, number in (("early", 3), ("middle", 4), ("late", 5), ("turned", 0))}
         for k in ("early", "middle"):
             second_pass(k, accs[k], 0)
             second_pass(k, accs[k], 1)

@@ -131,8 +131,8 @@ def tile_picked_haar_gelu_p_kernel(
                 )
             return acc
 
-        def gelu_by_channel(d, k, acc):
-            nc.scalar.activation(hidden[k][:, d], acc[:].rearrange("p t v -> p v t"), ACT.Gelu_apprx_tanh)
+        def gelu_by_channel(d, k, acc, pairs):
+            nc.scalar.activation(hidden[k][:, d, pairs], acc[:].rearrange("p t v -> p v t")[:, pairs], ACT.Gelu_apprx_tanh)
 
         def layer_by_patch(d, tiles, number):
             columns = slice(tiles.start * P, tiles.stop * P)
@@ -163,9 +163,9 @@ def tile_picked_haar_gelu_p_kernel(
                     stop=(not opens and t == PACK - 1),
                 )
 
-        def sums(k):
+        def sums(k, pairs):
             for b, op in enumerate((ALU.add, ALU.subtract)):
-                nc.vector.tensor_tensor(bands[k][:, b], hidden[k][:, 0], hidden[k][:, 1], op)
+                nc.vector.tensor_tensor(bands[k][:, b, pairs], hidden[k][:, 0, pairs], hidden[k][:, 1, pairs], op)
 
         def quantise(k, b):
             nc.vector.quantize_mx(
@@ -190,32 +190,40 @@ def tile_picked_haar_gelu_p_kernel(
             nc.scalar.activation(result[:], acc[:], ACT.Copy, scale=0.5)
             queue.dma_start(out=out[:, first_pair[k] : first_pair[k] + GROUP], in_=result[:])
 
-        low, high, both = slice(0, 1), slice(1, 2), slice(0, 2)
+        low, high = slice(0, 1), slice(1, 2)
+        whole, halves = slice(0, GROUP), (slice(0, GROUP // 2), slice(GROUP // 2, GROUP))
         first_rows = keep.tile([P, PACK, P], F32, name="first_rows", tag="first_rows", align_bytes=64)
         for number, tiles in enumerate((slice(0, 2), slice(2, 4))):
             gelu_by_patch(first_rows, tiles, layer_by_patch(0, tiles, number))
         negated_rows = keep.tile([P, PACK, P], F32, name="negated_rows", tag="negated_rows", align_bytes=64)
-        for d in range(2):
-            gelu_by_channel(d, "early", layer_by_channel(d, "early", 2 + d))
         nc.vector.tensor_scalar(negated_rows[:], first_rows[:], -1.0, None, ALU.mult)
-        sums("early")
-        gelu_by_channel(0, "middle", layer_by_channel(0, "middle", 4))
+        early_accs = [layer_by_channel(d, "early", 2 + d) for d in range(2)]
+        for pairs in halves:
+            for d in range(2):
+                gelu_by_channel(d, "early", early_accs[d], pairs)
+            sums("early", pairs)
+        quantise("early", low)
+        quantise("early", high)
+        gelu_by_channel(0, "middle", layer_by_channel(0, "middle", 4), whole)
         low_acc = bank(6, [P, PACK, GROUP])
         turn(low_acc, first_rows, True)
-        gelu_by_channel(1, "middle", layer_by_channel(1, "middle", 1))
-        sums("middle")
+        middle_acc = layer_by_channel(1, "middle", 1)
+        for pairs in halves:
+            gelu_by_channel(1, "middle", middle_acc, pairs)
+            sums("middle", pairs)
         second_rows = keep.tile([P, PACK, P], F32, name="second_rows", tag="second_rows", align_bytes=64)
         gelu_by_patch(second_rows, slice(0, 4), layer_by_patch(1, slice(0, 4), 2))
         high_acc = bank(7, [P, PACK, GROUP])
         turn(high_acc, negated_rows, True)
         late_accs = [layer_by_channel(d, "late", 3 + d) for d in range(2)]
-        quantise("early", both)
-        quantise("middle", both)
+        quantise("middle", low)
+        quantise("middle", high)
         turn(low_acc, second_rows, False)
         turn(high_acc, second_rows, False)
-        for d in range(2):
-            gelu_by_channel(d, "late", late_accs[d])
-        sums("late")
+        gelu_by_channel(0, "late", late_accs[0], whole)
+        for pairs in halves:
+            gelu_by_channel(1, "late", late_accs[1], pairs)
+            sums("late", pairs)
         accs = {k: bank(number, [N, GROUP]) for k, number in (("early", 3), ("middle", 4), ("late", 5), ("turned", 0))}
         for k in ("early", "middle"):
             second_pass(k, accs[k], 0)

@@ -24,9 +24,9 @@ VECTOR_QUADS = 24
 WARM_WIDTHS = (512, 512, 256)
 
 
-def load_scale_rows(queue, plane, rows):
+def load_scale_rows(queues, plane, rows):
     for r in range(4):
-        queue.dma_start(out=plane[r:P:32, :].bitcast(I32), in_=rows[r:16:4, :].bitcast(I32))
+        queues[r % len(queues)].dma_start(out=plane[r:P:32, :].bitcast(I32), in_=rows[r:16:4, :].bitcast(I32))
 
 
 def words_of(packed):
@@ -59,7 +59,7 @@ def tile_picked_haar_gelu_p_kernel(
         nc.vector.memset(picked_scales[:].bitcast(I32), 0)
         picked_rows = keep.tile([P, S], U8, name="picked_rows", align_bytes=64)
         nc.vector.tensor_copy(picked_rows[:], table_scales[:].indirect(offsets[:]))
-        load_scale_rows(nc.sync, picked_scales, picked_rows[32:96:4, :])
+        load_scale_rows([nc.sync, nc.scalar], picked_scales, picked_rows[32:96:4, :])
 
         identity = keep.tile([P, P], F32, name="identity", align_bytes=64)
         make_identity(nc, identity[:])
@@ -94,8 +94,8 @@ def tile_picked_haar_gelu_p_kernel(
         nc.sync.dma_start(out=band_w_words[:, 1, :], in_=words_of(w3_words))
         band_w_scales = reused.tile([P, 2 * N], U8, name="band_w_scales", offset=2 * N * 4, align_bytes=64)
         nc.gpsimd.memset(band_w_scales[:].bitcast(I32), 0)
-        load_scale_rows(nc.sync, band_w_scales[:, N:], w3_scales[0])
-        load_scale_rows(nc.sync, band_w_scales[:, :N], w2_scales[0])
+        load_scale_rows([nc.sync], band_w_scales[:, N:], w3_scales[0])
+        load_scale_rows([nc.sync], band_w_scales[:, :N], w2_scales[0])
 
         picked_words = {}
         for half in range(2):
@@ -198,9 +198,9 @@ def tile_picked_haar_gelu_p_kernel(
         negated_rows = keep.tile([P, PACK, P], F32, name="negated_rows", tag="negated_rows", align_bytes=64)
         nc.vector.tensor_scalar(negated_rows[:], first_rows[:], -1.0, None, ALU.mult)
         early_accs = [layer_by_channel(d, "early", 2 + d) for d in range(2)]
+        gelu_by_channel(0, "early", early_accs[0], whole)
         for pairs in halves:
-            for d in range(2):
-                gelu_by_channel(d, "early", early_accs[d], pairs)
+            gelu_by_channel(1, "early", early_accs[1], pairs)
             sums("early", pairs)
         quantise("early", low)
         quantise("early", high)
@@ -220,9 +220,9 @@ def tile_picked_haar_gelu_p_kernel(
         quantise("middle", high)
         turn(low_acc, second_rows, False)
         turn(high_acc, second_rows, False)
-        gelu_by_channel(0, "late", late_accs[0], whole)
         for pairs in halves:
-            gelu_by_channel(1, "late", late_accs[1], pairs)
+            for d in range(2):
+                gelu_by_channel(d, "late", late_accs[d], pairs)
             sums("late", pairs)
         accs = {k: bank(number, [N, GROUP]) for k, number in (("early", 3), ("middle", 4), ("late", 5), ("turned", 0))}
         for k in ("early", "middle"):
@@ -230,11 +230,10 @@ def tile_picked_haar_gelu_p_kernel(
             second_pass(k, accs[k], 1)
         for b, acc, sign in ((0, low_acc, 1.0), (1, high_acc, -1.0)):
             nc.scalar.activation(bands["turned"][:, b], acc[:].rearrange("p t v -> p v t"), ACT.Copy, scale=sign)
-        for b, band in enumerate((low, high)):
-            for k in ("turned", "late"):
-                quantise(k, band)
-                second_pass(k, accs[k], b)
+        for k, b in (("turned", 0), ("late", 0), ("late", 1), ("turned", 1)):
+            quantise(k, (low, high)[b])
+            second_pass(k, accs[k], b)
         store("early", accs["early"], nc.sync, "second_rows")
         store("middle", accs["middle"], nc.sync, "first_rows")
-        store("turned", accs["turned"], nc.sync, "result_turned")
-        store("late", accs["late"], nc.scalar, "result_late")
+        store("late", accs["late"], nc.sync, "result_late")
+        store("turned", accs["turned"], nc.scalar, "result_turned")

@@ -21,7 +21,7 @@ PACK = 4
 GROUP = 128
 QUARTER = 256
 VECTOR_QUADS = 24
-WARM_WIDTHS = (512, 512, 256)
+WARM_WIDTHS = (256, 256, 512, 256)
 
 
 def load_scale_rows(queues, plane, rows):
@@ -71,14 +71,16 @@ def tile_picked_haar_gelu_p_kernel(
         nc.scalar.copy(dealt[:, VECTOR_QUADS:], rows_by_quad[:, VECTOR_QUADS:])
         w1_codes = keep.tile([P, PACK * P], U32, name="w1_codes", align_bytes=64)
         w1_scales = keep.tile([P, PACK * P], U8, name="w1_scales", align_bytes=64)
-        nc.vector.quantize_mx(
-            out=w1_codes[:].bitcast(FP8X4),
-            scales=w1_scales[:],
-            in_=w1_grouped[:].rearrange("p t m j -> p (t m j)"),
-        )
+        for tiles in (slice(0, 2), slice(2, 4)):
+            columns = slice(tiles.start * P, tiles.stop * P)
+            nc.vector.quantize_mx(
+                out=w1_codes[:, columns].bitcast(FP8X4),
+                scales=w1_scales[:, columns],
+                in_=w1_grouped[:, tiles].rearrange("p t m j -> p (t m j)"),
+            )
 
         for turn_number, width in enumerate(WARM_WIDTHS):
-            idle = bank(5 + turn_number, [P, H])
+            idle = bank(4 + turn_number, [P, H])
             nc.tensor.matmul_mx(
                 out=idle[:, :width],
                 lhsT=w1_codes[:, :P].bitcast(FP8X4),

@@ -24,9 +24,9 @@ VECTOR_QUADS = 24
 WARM_WIDTHS = (256, 256, 512, 256)
 
 
-def load_scale_rows(queues, plane, rows):
+def load_scale_rows(queue, plane, rows):
     for r in range(4):
-        queues[r % len(queues)].dma_start(out=plane[r:P:32, :].bitcast(I32), in_=rows[r:16:4, :].bitcast(I32))
+        queue.dma_start(out=plane[r:P:32, :].bitcast(I32), in_=rows[r:16:4, :].bitcast(I32))
 
 
 def words_of(packed):
@@ -59,7 +59,7 @@ def tile_picked_haar_gelu_p_kernel(
         nc.vector.memset(picked_scales[:].bitcast(I32), 0)
         picked_rows = keep.tile([P, S], U8, name="picked_rows", align_bytes=64)
         nc.vector.tensor_copy(picked_rows[:], table_scales[:].indirect(offsets[:]))
-        load_scale_rows([nc.sync, nc.scalar], picked_scales, picked_rows[32:96:4, :])
+        load_scale_rows(nc.scalar, picked_scales, picked_rows[32:96:4, :])
 
         identity = keep.tile([P, P], F32, name="identity", align_bytes=64)
         make_identity(nc, identity[:])
@@ -96,8 +96,8 @@ def tile_picked_haar_gelu_p_kernel(
         nc.sync.dma_start(out=band_w_words[:, 1, :], in_=words_of(w3_words))
         band_w_scales = reused.tile([P, 2 * N], U8, name="band_w_scales", offset=2 * N * 4, align_bytes=64)
         nc.gpsimd.memset(band_w_scales[:].bitcast(I32), 0)
-        load_scale_rows([nc.sync], band_w_scales[:, N:], w3_scales[0])
-        load_scale_rows([nc.sync], band_w_scales[:, :N], w2_scales[0])
+        load_scale_rows(nc.sync, band_w_scales[:, N:], w3_scales[0])
+        load_scale_rows(nc.sync, band_w_scales[:, :N], w2_scales[0])
 
         picked_words = {}
         for half in range(2):

@@ -20,7 +20,7 @@ P = 128
 PACK = 4
 GROUP = 128
 QUARTER = 256
-VECTOR_QUADS = 24
+VECTOR_QUADS = 48
 WARM_WIDTHS = (256, 256, 512, 256)
 
 

@@ -21,7 +21,6 @@ PACK = 4
 GROUP = 128
 QUARTER = 256
 VECTOR_QUADS = 48
-WARM_WIDTHS = (256, 256, 512, 256)
 
 
 def load_scale_rows(queue, plane, rows):
@@ -77,18 +76,6 @@ def tile_picked_haar_gelu_p_kernel(
                 out=w1_codes[:, columns].bitcast(FP8X4),
                 scales=w1_scales[:, columns],
                 in_=w1_grouped[:, tiles].rearrange("p t m j -> p (t m j)"),
-            )
-
-        for turn_number, width in enumerate(WARM_WIDTHS):
-            idle = bank(4 + turn_number, [P, H])
-            nc.tensor.matmul_mx(
-                out=idle[:, :width],
-                lhsT=w1_codes[:, :P].bitcast(FP8X4),
-                lhsT_scale=w1_scales[:, :P],
-                rhs=w1_codes[:, :width].bitcast(FP8X4),
-                rhs_scale=w1_scales[:, :width],
-                start=True,
-                stop=True,
             )
 
         band_w_words = reused.tile([P, 2, N], I32, name="band_w_words", offset=0, align_bytes=64)

@@ -94,8 +94,9 @@ def tile_picked_haar_gelu_p_kernel(
                 entries = offsets[:, first // 16 : (first + QUARTER) // 16]
                 nc.vector.tensor_copy(picked_words[d, half][:], table_words[:].bitcast(U32).indirect(entries))
 
-        first_pair = {"turned": 0, "early": GROUP, "middle": 2 * GROUP, "late": 3 * GROUP}
-        hidden = {k: keep.tile([P, 2, GROUP, PACK], F32, name=f"hidden_{k}") for k in ("early", "middle", "late")}
+        first_pair = {"early": 0, "turned": GROUP, "middle": 2 * GROUP, "late": 3 * GROUP}
+        hidden = {k: keep.tile([P, 2, 2, GROUP, 2], F32, name=f"hidden_{k}") for k in ("early", "middle")}
+        hidden_late = keep.tile([P, 2, GROUP, PACK], F32, name="hidden_late")
         bands = {k: keep.tile([P, 2, GROUP, PACK], BF16, name=f"bands_{k}", align_bytes=64) for k in first_pair}
         codes = {k: keep.tile([P, 2, GROUP], U32, name=f"codes_{k}", align_bytes=64) for k in first_pair}
         scales = {k: keep.tile([P, 2, GROUP], U8, name=f"scales_{k}", align_bytes=64) for k in first_pair}
@@ -105,12 +106,12 @@ def tile_picked_haar_gelu_p_kernel(
             entry = d * V + first_pair[k]
             return picked_words[d, half][:, place : place + GROUP].bitcast(FP8X4), picked_scales[:, entry : entry + GROUP]
 
-        def layer_by_channel(d, k, number):
-            acc = bank(number, [P, PACK, GROUP])
+        def layer_by_channel(d, k, tiles, number):
+            acc = bank(number, [P, tiles.stop - tiles.start, GROUP])
             words, plane = patches(d, k)
-            for t in range(PACK):
+            for t in range(tiles.start, tiles.stop):
                 nc.tensor.matmul_mx(
-                    out=acc[:, t],
+                    out=acc[:, t - tiles.start],
                     lhsT=w1_codes[:, t * P : (t + 1) * P].bitcast(FP8X4),
                     lhsT_scale=w1_scales[:, t * P : (t + 1) * P],
                     rhs=words,
@@ -120,8 +121,8 @@ def tile_picked_haar_gelu_p_kernel(
                 )
             return acc
 
-        def gelu_by_channel(d, k, acc, pairs):
-            nc.scalar.activation(hidden[k][:, d, pairs], acc[:].rearrange("p t v -> p v t")[:, pairs], ACT.Gelu_apprx_tanh)
+        def gelu_by_channel(target, acc, pairs):
+            nc.scalar.activation(target[:, pairs], acc[:].rearrange("p t v -> p v t")[:, pairs], ACT.Gelu_apprx_tanh)
 
         def layer_by_patch(d, tiles, number):
             columns = slice(tiles.start * P, tiles.stop * P)
@@ -153,8 +154,12 @@ def tile_picked_haar_gelu_p_kernel(
                 )
 
         def sums(k, pairs):
+            if k == "late":
+                pieces = [hidden_late[:, d, pairs].rearrange("p v (h u) -> p v h u", u=2) for d in range(2)]
+            else:
+                pieces = [hidden[k][:, d].rearrange("p h v u -> p v h u")[:, pairs] for d in range(2)]
             for b, op in enumerate((ALU.add, ALU.subtract)):
-                nc.vector.tensor_tensor(bands[k][:, b, pairs], hidden[k][:, 0, pairs], hidden[k][:, 1, pairs], op)
+                nc.vector.tensor_tensor(bands[k][:, b, pairs].rearrange("p v (h u) -> p v h u", u=2), pieces[0], pieces[1], op)
 
         def quantise(k, b):
             nc.vector.quantize_mx(
@@ -179,41 +184,39 @@ def tile_picked_haar_gelu_p_kernel(
             nc.scalar.activation(result[:], acc[:], ACT.Copy, scale=0.5)
             queue.dma_start(out=out[:, first_pair[k] : first_pair[k] + GROUP], in_=result[:])
 
-        low, high = slice(0, 1), slice(1, 2)
+        low, high, both = slice(0, 1), slice(1, 2), slice(0, 2)
         whole, halves = slice(0, GROUP), (slice(0, GROUP // 2), slice(GROUP // 2, GROUP))
+        tile_pairs = (slice(0, 2), slice(2, 4))
+        for d in range(2):
+            for h, tiles in enumerate(tile_pairs):
+                gelu_by_channel(hidden["early"][:, d, h], layer_by_channel(d, "early", tiles, 2 * d + h), whole)
+        sums("early", whole)
         first_rows = keep.tile([P, PACK, P], F32, name="first_rows", tag="first_rows", align_bytes=64)
-        for number, tiles in enumerate((slice(0, 2), slice(2, 4))):
-            gelu_by_patch(first_rows, tiles, layer_by_patch(0, tiles, number))
+        for h, tiles in enumerate(tile_pairs):
+            gelu_by_patch(first_rows, tiles, layer_by_patch(0, tiles, 4 + h))
         negated_rows = keep.tile([P, PACK, P], F32, name="negated_rows", tag="negated_rows", align_bytes=64)
         nc.vector.tensor_scalar(negated_rows[:], first_rows[:], -1.0, None, ALU.mult)
-        early_accs = [layer_by_channel(d, "early", 2 + d) for d in range(2)]
-        gelu_by_channel(0, "early", early_accs[0], whole)
-        for pairs in halves:
-            gelu_by_channel(1, "early", early_accs[1], pairs)
-            sums("early", pairs)
-        quantise("early", low)
-        quantise("early", high)
-        gelu_by_channel(0, "middle", layer_by_channel(0, "middle", 4), whole)
-        low_acc = bank(6, [P, PACK, GROUP])
-        turn(low_acc, first_rows, True)
-        middle_acc = layer_by_channel(1, "middle", 1)
-        for pairs in halves:
-            gelu_by_channel(1, "middle", middle_acc, pairs)
-            sums("middle", pairs)
+        quantise("early", both)
+        for d in range(2):
+            for h, tiles in enumerate(tile_pairs):
+                gelu_by_channel(hidden["middle"][:, d, h], layer_by_channel(d, "middle", tiles, (6 + 2 * d + h) % 8), whole)
+        sums("middle", whole)
         second_rows = keep.tile([P, PACK, P], F32, name="second_rows", tag="second_rows", align_bytes=64)
         gelu_by_patch(second_rows, slice(0, 4), layer_by_patch(1, slice(0, 4), 2))
-        high_acc = bank(7, [P, PACK, GROUP])
-        turn(high_acc, negated_rows, True)
-        late_accs = [layer_by_channel(d, "late", 3 + d) for d in range(2)]
+        late_accs = [layer_by_channel(d, "late", slice(0, 4), number) for d, number in enumerate((7, 0))]
         quantise("middle", low)
         quantise("middle", high)
+        low_acc = bank(1, [P, PACK, GROUP])
+        turn(low_acc, first_rows, True)
         turn(low_acc, second_rows, False)
+        high_acc = bank(2, [P, PACK, GROUP])
+        turn(high_acc, negated_rows, True)
         turn(high_acc, second_rows, False)
         for pairs in halves:
             for d in range(2):
-                gelu_by_channel(d, "late", late_accs[d], pairs)
+                gelu_by_channel(hidden_late[:, d], late_accs[d], pairs)
             sums("late", pairs)
-        accs = {k: bank(number, [N, GROUP]) for k, number in (("early", 3), ("middle", 4), ("late", 5), ("turned", 0))}
+        accs = {k: bank(number, [N, GROUP]) for k, number in (("early", 7), ("middle", 0), ("late", 5), ("turned", 6))}
         for k in ("early", "middle"):
             second_pass(k, accs[k], 0)
             second_pass(k, accs[k], 1)

@@ -58,7 +58,7 @@ def tile_picked_haar_gelu_p_kernel(
         nc.vector.memset(picked_scales[:].bitcast(I32), 0)
         picked_rows = keep.tile([P, S], U8, name="picked_rows", align_bytes=64)
         nc.vector.tensor_copy(picked_rows[:], table_scales[:].indirect(offsets[:]))
-        load_scale_rows(nc.scalar, picked_scales, picked_rows[32:96:4, :])
+        load_scale_rows(nc.sync, picked_scales, picked_rows[32:96:4, :])
 
         identity = keep.tile([P, P], F32, name="identity", align_bytes=64)
         make_identity(nc, identity[:])
@@ -94,7 +94,7 @@ def tile_picked_haar_gelu_p_kernel(
                 entries = offsets[:, first // 16 : (first + QUARTER) // 16]
                 nc.vector.tensor_copy(picked_words[d, half][:], table_words[:].bitcast(U32).indirect(entries))
 
-        first_pair = {"early": 0, "turned": GROUP, "middle": 2 * GROUP, "late": 3 * GROUP}
+        first_pair = {"early": 0, "middle": GROUP, "turned": 2 * GROUP, "late": 3 * GROUP}
         hidden = {k: keep.tile([P, 2, 2, GROUP, 2], F32, name=f"hidden_{k}") for k in ("early", "middle")}
         hidden_late = keep.tile([P, 2, GROUP, PACK], F32, name="hidden_late")
         bands = {k: keep.tile([P, 2, GROUP, PACK], BF16, name=f"bands_{k}", align_bytes=64) for k in first_pair}
@@ -153,13 +153,17 @@ def tile_picked_haar_gelu_p_kernel(
                     stop=(not opens and t == PACK - 1),
                 )
 
-        def sums(k, pairs):
+        def band_sum(k, pairs, b):
             if k == "late":
                 pieces = [hidden_late[:, d, pairs].rearrange("p v (h u) -> p v h u", u=2) for d in range(2)]
             else:
                 pieces = [hidden[k][:, d].rearrange("p h v u -> p v h u")[:, pairs] for d in range(2)]
-            for b, op in enumerate((ALU.add, ALU.subtract)):
-                nc.vector.tensor_tensor(bands[k][:, b, pairs].rearrange("p v (h u) -> p v h u", u=2), pieces[0], pieces[1], op)
+            op = (ALU.add, ALU.subtract)[b]
+            nc.vector.tensor_tensor(bands[k][:, b, pairs].rearrange("p v (h u) -> p v h u", u=2), pieces[0], pieces[1], op)
+
+        def sums(k, pairs):
+            band_sum(k, pairs, 0)
+            band_sum(k, pairs, 1)
 
         def quantise(k, b):
             nc.vector.quantize_mx(
@@ -187,36 +191,39 @@ def tile_picked_haar_gelu_p_kernel(
         low, high, both = slice(0, 1), slice(1, 2), slice(0, 2)
         whole, halves = slice(0, GROUP), (slice(0, GROUP // 2), slice(GROUP // 2, GROUP))
         tile_pairs = (slice(0, 2), slice(2, 4))
+        for d, h in ((0, 0), (0, 1), (1, 0)):
+            gelu_by_channel(hidden["early"][:, d, h], layer_by_channel(d, "early", tile_pairs[h], 2 * d + h), whole)
+        early_acc = layer_by_channel(1, "early", tile_pairs[1], 3)
+        for pairs in halves:
+            gelu_by_channel(hidden["early"][:, 1, 1], early_acc, pairs)
+            sums("early", pairs)
         for d in range(2):
             for h, tiles in enumerate(tile_pairs):
-                gelu_by_channel(hidden["early"][:, d, h], layer_by_channel(d, "early", tiles, 2 * d + h), whole)
-        sums("early", whole)
+                gelu_by_channel(hidden["middle"][:, d, h], layer_by_channel(d, "middle", tiles, 4 + 2 * d + h), whole)
+        quantise("early", low)
+        band_sum("middle", whole, 0)
+        quantise("early", high)
+        band_sum("middle", whole, 1)
         first_rows = keep.tile([P, PACK, P], F32, name="first_rows", tag="first_rows", align_bytes=64)
         for h, tiles in enumerate(tile_pairs):
-            gelu_by_patch(first_rows, tiles, layer_by_patch(0, tiles, 4 + h))
+            gelu_by_patch(first_rows, tiles, layer_by_patch(0, tiles, h))
         negated_rows = keep.tile([P, PACK, P], F32, name="negated_rows", tag="negated_rows", align_bytes=64)
         nc.vector.tensor_scalar(negated_rows[:], first_rows[:], -1.0, None, ALU.mult)
-        quantise("early", both)
-        for d in range(2):
-            for h, tiles in enumerate(tile_pairs):
-                gelu_by_channel(hidden["middle"][:, d, h], layer_by_channel(d, "middle", tiles, (6 + 2 * d + h) % 8), whole)
-        sums("middle", whole)
         second_rows = keep.tile([P, PACK, P], F32, name="second_rows", tag="second_rows", align_bytes=64)
         gelu_by_patch(second_rows, slice(0, 4), layer_by_patch(1, slice(0, 4), 2))
-        late_accs = [layer_by_channel(d, "late", slice(0, 4), number) for d, number in enumerate((7, 0))]
-        quantise("middle", low)
-        quantise("middle", high)
-        low_acc = bank(1, [P, PACK, GROUP])
+        late_accs = [layer_by_channel(d, "late", slice(0, 4), d) for d in range(2)]
+        quantise("middle", both)
+        low_acc = bank(3, [P, PACK, GROUP])
         turn(low_acc, first_rows, True)
         turn(low_acc, second_rows, False)
-        high_acc = bank(2, [P, PACK, GROUP])
-        turn(high_acc, negated_rows, True)
-        turn(high_acc, second_rows, False)
+        high_acc = bank(4, [P, PACK, GROUP])
+        turn(high_acc, second_rows, True)
+        turn(high_acc, negated_rows, False)
         for pairs in halves:
             for d in range(2):
                 gelu_by_channel(hidden_late[:, d], late_accs[d], pairs)
             sums("late", pairs)
-        accs = {k: bank(number, [N, GROUP]) for k, number in (("early", 7), ("middle", 0), ("late", 5), ("turned", 6))}
+        accs = {k: bank(number, [N, GROUP]) for k, number in (("early", 0), ("middle", 1), ("late", 5), ("turned", 6))}
         for k in ("early", "middle"):
             second_pass(k, accs[k], 0)
             second_pass(k, accs[k], 1)
@@ -225,7 +232,7 @@ def tile_picked_haar_gelu_p_kernel(
         for k, b in (("turned", 0), ("late", 0), ("late", 1), ("turned", 1)):
             quantise(k, (low, high)[b])
             second_pass(k, accs[k], b)
-        store("early", accs["early"], nc.sync, "second_rows")
-        store("middle", accs["middle"], nc.sync, "first_rows")
+        store("early", accs["early"], nc.sync, "negated_rows")
+        store("middle", accs["middle"], nc.sync, "second_rows")
         store("late", accs["late"], nc.sync, "result_late")
         store("turned", accs["turned"], nc.scalar, "result_turned")

@@ -58,7 +58,7 @@ def tile_picked_haar_gelu_p_kernel(
         nc.vector.memset(picked_scales[:].bitcast(I32), 0)
         picked_rows = keep.tile([P, S], U8, name="picked_rows", align_bytes=64)
         nc.vector.tensor_copy(picked_rows[:], table_scales[:].indirect(offsets[:]))
-        load_scale_rows(nc.sync, picked_scales, picked_rows[32:96:4, :])
+        load_scale_rows(nc.scalar, picked_scales, picked_rows[32:96:4, :])
 
         identity = keep.tile([P, P], F32, name="identity", align_bytes=64)
         make_identity(nc, identity[:])

@@ -201,9 +201,8 @@ def tile_picked_haar_gelu_p_kernel(
             for h, tiles in enumerate(tile_pairs):
                 gelu_by_channel(hidden["middle"][:, d, h], layer_by_channel(d, "middle", tiles, 4 + 2 * d + h), whole)
         quantise("early", low)
-        band_sum("middle", whole, 0)
         quantise("early", high)
-        band_sum("middle", whole, 1)
+        sums("middle", whole)
         first_rows = keep.tile([P, PACK, P], F32, name="first_rows", tag="first_rows", align_bytes=64)
         for h, tiles in enumerate(tile_pairs):
             gelu_by_patch(first_rows, tiles, layer_by_patch(0, tiles, h))

from contextlib import ExitStack

import concourse.mybir as mybir
from concourse.masks import make_identity

K, T, S, V, H, N = 512, 4096, 1024, 512, 512, 128
FLOPS = 2 * K * H * S + 2 * 2 * H * N * V

F32 = mybir.dt.float32
BF16 = mybir.dt.bfloat16
I32 = mybir.dt.int32
U32 = mybir.dt.uint32
U16 = mybir.dt.uint16
U8 = mybir.dt.uint8
FP8X4 = mybir.dt.float8_e4m3fn_x4
ACT = mybir.ActivationFunctionType
ALU = mybir.AluOpType

P = 128
PACK = 4
GROUP = 128
QUARTER = 256
VECTOR_QUADS = 48


def load_scale_rows(queue, plane, rows):
    for r in range(4):
        queue.dma_start(out=plane[r:P:32, :].bitcast(I32), in_=rows[r:16:4, :].bitcast(I32))


def words_of(packed):
    return packed[0].rearrange("p n t -> p (n t)").bitcast(I32)


def tile_picked_haar_gelu_p_kernel(
    tc, x_words, x_scales, w1, w2_words, w2_scales, w3_words, w3_scales, offs, out
):
    nc = tc.nc
    with ExitStack() as ctx:
        keep = ctx.enter_context(tc.tile_pool(name="keep", bufs=1))
        reused = ctx.enter_context(tc.tile_pool(name="reused", bufs=1))
        psum = ctx.enter_context(tc.psum_pool(name="psum", bufs=1))

        def bank(number, shape):
            return psum.tile(shape, F32, name=f"bank{number}", tag=f"bank{number}")

        w1_raw = keep.tile([P, PACK, H], F32, name="w1_raw", align_bytes=64)
        nc.sync.dma_start(out=w1_raw[:], in_=w1.rearrange("(p j) c -> p j c", j=PACK))
        offsets = keep.tile([P, S // 16], U16, name="offsets")
        nc.sync.dma_start(offsets[:], offs)
        table_scales = reused.tile([P, T], U8, name="table_scales", offset=0, align_bytes=64)
        nc.vector.memset(table_scales[:].bitcast(I32), 0)
        nc.sync.dma_start(out=table_scales[32:96:4, :].bitcast(I32), in_=x_scales[0].bitcast(I32))
        table_words = keep.tile([P, T], I32, name="table_words", align_bytes=64)
        nc.sync.dma_start(out=table_words[:], in_=words_of(x_words))

        picked_scales = keep.tile([P, S], U8, name="picked_scales", align_bytes=64)
        nc.vector.memset(picked_scales[:].bitcast(I32), 0)
        picked_rows = keep.tile([P, S], U8, name="picked_rows", align_bytes=64)
        nc.vector.tensor_copy(picked_rows[:], table_scales[:].indirect(offsets[:]))
        load_scale_rows(nc.scalar, picked_scales, picked_rows[32:96:4, :])

        identity = keep.tile([P, P], F32, name="identity", align_bytes=64)
        make_identity(nc, identity[:])

        w1_grouped = keep.tile([P, PACK, P, PACK], BF16, name="w1_grouped", align_bytes=64)
        dealt = w1_grouped[:].rearrange("p t m j -> p m t j")
        rows_by_quad = w1_raw[:].rearrange("p j (m t) -> p m t j", t=PACK)
        nc.vector.tensor_copy(dealt[:, :VECTOR_QUADS], rows_by_quad[:, :VECTOR_QUADS])
        nc.scalar.copy(dealt[:, VECTOR_QUADS:], rows_by_quad[:, VECTOR_QUADS:])
        w1_codes = keep.tile([P, PACK * P], U32, name="w1_codes", align_bytes=64)
        w1_scales = keep.tile([P, PACK * P], U8, name="w1_scales", align_bytes=64)
        for tiles in (slice(0, 2), slice(2, 4)):
            columns = slice(tiles.start * P, tiles.stop * P)
            nc.vector.quantize_mx(
                out=w1_codes[:, columns].bitcast(FP8X4),
                scales=w1_scales[:, columns],
                in_=w1_grouped[:, tiles].rearrange("p t m j -> p (t m j)"),
            )

        band_w_words = reused.tile([P, 2, N], I32, name="band_w_words", offset=0, align_bytes=64)
        nc.sync.dma_start(out=band_w_words[:, 0, :], in_=words_of(w2_words))
        nc.sync.dma_start(out=band_w_words[:, 1, :], in_=words_of(w3_words))
        band_w_scales = reused.tile([P, 2 * N], U8, name="band_w_scales", offset=2 * N * 4, align_bytes=64)
        nc.gpsimd.memset(band_w_scales[:].bitcast(I32), 0)
        load_scale_rows(nc.sync, band_w_scales[:, N:], w3_scales[0])
        load_scale_rows(nc.sync, band_w_scales[:, :N], w2_scales[0])

        picked_words = {}
        for half in range(2):
            for d in range(2):
                first = d * V + half * QUARTER
                picked_words[d, half] = keep.tile([P, QUARTER], U32, name=f"picked_words_{d}{half}", align_bytes=64)
                entries = offsets[:, first // 16 : (first + QUARTER) // 16]
                nc.vector.tensor_copy(picked_words[d, half][:], table_words[:].bitcast(U32).indirect(entries))

        first_pair = {"early": 0, "middle": GROUP, "turned": 2 * GROUP, "late": 3 * GROUP}
        hidden = {k: keep.tile([P, 2, 2, GROUP, 2], F32, name=f"hidden_{k}") for k in ("early", "middle")}
        hidden_late = keep.tile([P, 2, GROUP, PACK], F32, name="hidden_late")
        bands = {k: keep.tile([P, 2, GROUP, PACK], BF16, name=f"bands_{k}", align_bytes=64) for k in first_pair}
        codes = {k: keep.tile([P, 2, GROUP], U32, name=f"codes_{k}", align_bytes=64) for k in first_pair}
        scales = {k: keep.tile([P, 2, GROUP], U8, name=f"scales_{k}", align_bytes=64) for k in first_pair}

        def patches(d, k):
            half, place = divmod(first_pair[k], QUARTER)
            entry = d * V + first_pair[k]
            return picked_words[d, half][:, place : place + GROUP].bitcast(FP8X4), picked_scales[:, entry : entry + GROUP]

        def layer_by_channel(d, k, tiles, number):
            acc = bank(number, [P, tiles.stop - tiles.start, GROUP])
            words, plane = patches(d, k)
            for t in range(tiles.start, tiles.stop):
                nc.tensor.matmul_mx(
                    out=acc[:, t - tiles.start],
                    lhsT=w1_codes[:, t * P : (t + 1) * P].bitcast(FP8X4),
                    lhsT_scale=w1_scales[:, t * P : (t + 1) * P],
                    rhs=words,
                    rhs_scale=plane,
                    start=True,
                    stop=True,
                )
            return acc

        def gelu_by_channel(target, acc, pairs):
            nc.scalar.activation(target[:, pairs], acc[:].rearrange("p t v -> p v t")[:, pairs], ACT.Gelu_apprx_tanh)

        def layer_by_patch(d, tiles, number):
            columns = slice(tiles.start * P, tiles.stop * P)
            acc = bank(number, [P, columns.stop - columns.start])
            words, plane = patches(d, "turned")
            nc.tensor.matmul_mx(
                out=acc[:],
                lhsT=words,
                lhsT_scale=plane,
                rhs=w1_codes[:, columns].bitcast(FP8X4),
                rhs_scale=w1_scales[:, columns],
                start=True,
                stop=True,
            )
            return acc

        def gelu_by_patch(rows, tiles, acc):
            nc.scalar.activation(rows[:, tiles].rearrange("v t m -> v (t m)"), acc[:], ACT.Gelu_apprx_tanh)

        def turn(acc, rows, opens):
            for t in range(PACK):
                nc.tensor.matmul(
                    acc[:, t],
                    rows[:, t],
                    identity[:],
                    is_transpose=True,
                    start=(opens and t == 0),
                    stop=(not opens and t == PACK - 1),
                )

        def band_sum(k, pairs, b):
            if k == "late":
                pieces = [hidden_late[:, d, pairs].rearrange("p v (h u) -> p v h u", u=2) for d in range(2)]
            else:
                pieces = [hidden[k][:, d].rearrange("p h v u -> p v h u")[:, pairs] for d in range(2)]
            op = (ALU.add, ALU.subtract)[b]
            nc.vector.tensor_tensor(bands[k][:, b, pairs].rearrange("p v (h u) -> p v h u", u=2), pieces[0], pieces[1], op)

        def sums(k, pairs):
            band_sum(k, pairs, 0)
            band_sum(k, pairs, 1)

        def quantise(k, b):
            nc.vector.quantize_mx(
                out=codes[k][:, b].rearrange("p b v -> p (b v)").bitcast(FP8X4),
                scales=scales[k][:, b].rearrange("p b v -> p (b v)"),
                in_=bands[k][:, b].rearrange("p b v t -> p (b v t)"),
            )

        def second_pass(k, acc, b):
            nc.tensor.matmul_mx(
                out=acc[:],
                lhsT=band_w_words[:, b, :].bitcast(FP8X4),
                lhsT_scale=band_w_scales[:, b * N : (b + 1) * N],
                rhs=codes[k][:, b].bitcast(FP8X4),
                rhs_scale=scales[k][:, b],
                start=(b == 0),
                stop=(b == 1),
            )

        def store(k, acc, queue, tag):
            result = keep.tile([N, GROUP], F32, name=f"result_{k}", tag=tag, align_bytes=64)
            nc.scalar.activation(result[:], acc[:], ACT.Copy, scale=0.5)
            queue.dma_start(out=out[:, first_pair[k] : first_pair[k] + GROUP], in_=result[:])

        low, high, both = slice(0, 1), slice(1, 2), slice(0, 2)
        whole, halves = slice(0, GROUP), (slice(0, GROUP // 2), slice(GROUP // 2, GROUP))
        tile_pairs = (slice(0, 2), slice(2, 4))
        for d, h in ((0, 0), (0, 1), (1, 0)):
            gelu_by_channel(hidden["early"][:, d, h], layer_by_channel(d, "early", tile_pairs[h], 2 * d + h), whole)
        early_acc = layer_by_channel(1, "early", tile_pairs[1], 3)
        for pairs in halves:
            gelu_by_channel(hidden["early"][:, 1, 1], early_acc, pairs)
            sums("early", pairs)
        for d in range(2):
            for h, tiles in enumerate(tile_pairs):
                gelu_by_channel(hidden["middle"][:, d, h], layer_by_channel(d, "middle", tiles, 4 + 2 * d + h), whole)
        quantise("early", low)
        quantise("early", high)
        sums("middle", whole)
        first_rows = keep.tile([P, PACK, P], F32, name="first_rows", tag="first_rows", align_bytes=64)
        for h, tiles in enumerate(tile_pairs):
            gelu_by_patch(first_rows, tiles, layer_by_patch(0, tiles, h))
        negated_rows = keep.tile([P, PACK, P], F32, name="negated_rows", tag="negated_rows", align_bytes=64)
        nc.vector.tensor_scalar(negated_rows[:], first_rows[:], -1.0, None, ALU.mult)
        second_rows = keep.tile([P, PACK, P], F32, name="second_rows", tag="second_rows", align_bytes=64)
        gelu_by_patch(second_rows, slice(0, 4), layer_by_patch(1, slice(0, 4), 2))
        late_accs = [layer_by_channel(d, "late", slice(0, 4), d) for d in range(2)]
        quantise("middle", both)
        low_acc = bank(3, [P, PACK, GROUP])
        turn(low_acc, first_rows, True)
        turn(low_acc, second_rows, False)
        high_acc = bank(4, [P, PACK, GROUP])
        turn(high_acc, second_rows, True)
        turn(high_acc, negated_rows, False)
        for pairs in halves:
            for d in range(2):
                gelu_by_channel(hidden_late[:, d], late_accs[d], pairs)
            sums("late", pairs)
        accs = {k: bank(number, [N, GROUP]) for k, number in (("early", 0), ("middle", 1), ("late", 5), ("turned", 6))}
        for k in ("early", "middle"):
            second_pass(k, accs[k], 0)
            second_pass(k, accs[k], 1)
        for b, acc, sign in ((0, low_acc, 1.0), (1, high_acc, -1.0)):
            nc.scalar.activation(bands["turned"][:, b], acc[:].rearrange("p t v -> p v t"), ACT.Copy, scale=sign)
        for k, b in (("turned", 0), ("late", 0), ("late", 1), ("turned", 1)):
            quantise(k, (low, high)[b])
            second_pass(k, accs[k], b)
        store("early", accs["early"], nc.sync, "negated_rows")
        store("middle", accs["middle"], nc.sync, "second_rows")
        store("late", accs["late"], nc.sync, "result_late")
        store("turned", accs["turned"], nc.scalar, "result_turned")
